import numpy as np, ml_dtypes
CORES = [35,38,43,46]
N = 4
BF = ml_dtypes.bfloat16
def gentries(a):
    return np.ascontiguousarray(a.reshape(8, 16, -1).transpose(0, 2, 1)).reshape(8, -1)
def gtable(e):
    e = np.asarray(e); return np.ascontiguousarray(e.reshape(8, -1, 16).transpose(0, 2, 1)).reshape(128, -1).astype(np.int32)
V, G, R, CAP, L, RO = 3136, 320, 1024, 256, 3, 2
W = V + (N - 1) * G
def full(p):
    return np.concatenate([p, np.broadcast_to(np.arange(V, W), (N, 8, W - V))], axis=2).astype(np.int64)
def reach(t, p):
    m = t; q = p
    for i in range(L):
        m = np.maximum(m, np.take_along_axis(m, q[:, :, None, :], 3)); q = np.take_along_axis(q, q, 2)
    return m
def pointers(rng, stay):
    p = rng.integers(0, W, (N, 8, V))
    return np.where(rng.random((N, 8, V)) < stay, np.arange(V), p)
def base(rng):
    x = (256 * rng.random((N, 8, 16, W)) * rng.random((N, 8, 1, W))).astype(np.int32)
    return x, pointers(rng, 0.3), pointers(rng, 0.3), rng.integers(0, W, (N, 8, 16, R)), rng.integers(0, V, (N, 8, N - 1, G))
def both(x, up, lo):
    return reach(x, full(up))[..., :V], reach(x, full(lo))[..., :V]
def witness(rng, mu, ml):
    s = mu.shape; w = np.where(rng.random(s) < rng.random((N, 8, 1, V)), mu, ml) + rng.integers(-6, 7, s)
    w = w + np.where(rng.random((N, 8, 1, V)) < 0.3, rng.integers(-120, 121, s), 0)
    return np.minimum(np.maximum(w, 0), 255)
def bar(mu, ml, w, n):
    d = np.add.reduce(np.abs(mu - w), axis=2) + np.add.reduce(np.abs(ml - w), axis=2)
    return np.take_along_axis(np.sort(d, axis=2), V - 1 - n[:, :, None], 2)[:, :, 0]
def pack(x, w, th, up, lo, rl, snd):
    return {"x": np.ascontiguousarray(x.reshape(N, 128, W)).astype(np.float32).astype(BF), "w": np.ascontiguousarray(w.reshape(N, 128, V)).astype(np.float32).astype(BF),
            "th": np.repeat(th, 16, axis=1).reshape(N, 128, 1).astype(np.int32), "up": np.stack([gtable(a) for a in up]), "lo": np.stack([gtable(a) for a in lo]),
            "rl": np.ascontiguousarray(rl.reshape(N, 128, R)).astype(np.int32), "snd": np.stack([gtable(a.reshape(8, -1)) for a in snd])}
def setup_inputs(rng):
    x, up, lo, rl, snd = base(rng); mu, ml = both(x, up, lo); w = witness(rng, mu, ml)
    n = rng.choice(np.array([CAP // 4, CAP - 8, 2 * CAP, 4 * CAP]), (N, 8))
    return pack(x, w, bar(mu, ml, w, n), up, lo, rl, snd)
def setup_inputs_room(rng):
    x, up, lo, rl, snd = base(rng); mu = reach(x, full(up))[..., :V]
    n = rng.choice(np.array([0, 1, CAP - 1, CAP, CAP + 1, V]), (N, 8)); n[0] = (CAP, CAP + 1, V, CAP - 1, 1, 0, CAP, CAP + 1); n[1, 0] = CAP
    mark = np.argsort(rng.random((N, 8, V)), axis=2) < n[:, :, None]
    off = np.where(mark[:, :, None, :], rng.integers(20, 91, mu.shape), rng.integers(0, 4, mu.shape))
    return pack(x, np.where(mu < 128, mu + off, mu - off), rng.integers(100, 600, (N, 8)), up, up, rl, snd)
def setup_inputs_alike(rng):
    x, up, lo, rl, snd = base(rng); ends = np.array([0, 3, V - 1, V, W - 1])
    x = np.take_along_axis(rng.integers(0, 256, (N, 8, 16, 6)), rng.integers(0, 6, (N, 8, 1, W)), 3).astype(np.int32)
    up = pointers(rng, 0.6); lo = pointers(rng, 0.6)
    up[:, 1::2] = np.where(rng.random((N, 4, V)) < 0.5, rng.choice(ends, (N, 4, V)), up[:, 1::2]); lo[:, ::4] = rng.choice(ends, (N, 2, V))
    rl[:, 2:6] = np.tile(rl[:, 2:6, :4], (1, 1, 4, 1)); rl[:, 6] = rng.choice(ends, (N, 16, R)); rl[:, 7] = rl[:, 7, :1]
    snd[:, ::2] = rng.choice(np.array([0, 3, V - 2, V - 1]), (N, 4, N - 1, G))
    mu, ml = both(x, up, lo); w = witness(rng, mu, ml); n = rng.choice(np.array([CAP // 2, CAP, 2 * CAP]), (N, 8))
    return pack(x, w, bar(mu, ml, w, n), up, lo, rl, snd)
def setup_inputs_deep(rng):
    x, up, lo, rl, snd = base(rng)
    x = (rng.integers(0, 16, x.shape) + np.where(rng.random((N, 8, 1, W)) * 12 < 1, rng.integers(0, 240, x.shape), 0)).astype(np.int32)
    for c in (0, V - 1, V, W - 1): x[..., c] = rng.integers(0, 256, (N, 8, 16))
    up[:, ::2] = (np.arange(V) + 1) % V
    o = np.argsort(rng.random((N, 4, V)), axis=2); p = np.empty_like(o); np.put_along_axis(p, o, np.roll(o, -1, axis=2), 2); up[:, 1::2] = p
    lo = pointers(rng, 0.0); lo[:, ::3] = np.maximum(np.arange(V) - 1, 0); lo[:, 1, V - 1] = W - 1; lo[:, 2, 0] = V
    mu, ml = both(x, up, lo); w = witness(rng, mu, ml); n = rng.choice(np.array([CAP // 2, CAP, 3 * CAP]), (N, 8))
    return pack(x, w, bar(mu, ml, w, n), up, lo, rl, snd)
def setup_inputs_crowd(rng):
    x, up, lo, rl, snd = base(rng); own = np.arange(V); m = np.argsort(rng.random((N, 8, V)), axis=2); w = np.zeros((N, 8, 16, V), np.int64)
    lo[:, :2] = up[:, :2]; mark = own % 16 == rng.integers(0, 16, (N, 2, 1))
    mu = reach(x[:, :2], full(up)[:, :2])[..., :V]
    off = np.where(mark[:, :, None, :], rng.integers(20, 91, mu.shape), rng.integers(0, 4, mu.shape))
    w[:, :2] = np.where(mu < 128, mu + off, mu - off)
    for a in range(N):
        for g in (2, 3, 4, 5, 7):
            b = 37 if g < 4 else 1; n = CAP if g in (2, 7) else int(rng.choice(np.array([CAP, CAP + 1, V // 2])))
            big = np.flatnonzero(m[a, g] >= V - b); hit = m[a, g] < n
            x[a, g] = x[a, g] * 5 // 8; x[a, g][:, big] = rng.integers(201, 256, (16, b))
            if g == 7:
                zero = np.flatnonzero((m[a, g] >= V - 65) & (m[a, g] < V - 1)); x[a, g][:, zero] = 0; rl[a, g] = rng.choice(zero, (16, R))
            lo[a, g] = np.where(hit, rng.choice(big, V), own)
            go = hit & (g < 7)
            up[a, g] = np.where(go & ~np.isin(up[a, g], big), up[a, g], own)
            mine = x[a, g][:, :V]
            w[a, g] = np.where(go, (mine * rng.random(mine.shape)).astype(np.int64), mine)
            if g == 5:
                p = up[a, g].copy(); up[a, g] = lo[a, g]; lo[a, g] = p
    far = np.zeros((N, 8, 1, 1), bool); far[:, 6] = True; far[int(rng.integers(0, N))] = True
    x = np.where(far, 200 + x * 55 // 255, x); w = np.where(far, rng.integers(0, 31, w.shape), w)
    return pack(x, w, rng.integers(100, 600, (N, 8)), up, lo, rl, snd)
def setup_inputs_spread(rng):
    x, up, lo, rl, snd = base(rng)
    cs = np.exp2(8 * rng.random((N, 8, 1, W))) * (rng.random((N, 8, 1, W)) > 0.0625)
    x = np.minimum((cs * rng.random(x.shape)).astype(np.int32), 255)
    up = pointers(rng, rng.choice(np.array([0.0, 0.1, 0.5, 0.9]), (N, 8, 1))); lo = pointers(rng, rng.choice(np.array([0.0, 0.1, 0.5, 0.9]), (N, 8, 1)))
    mu, ml = both(x, up, lo)
    w = np.where(rng.random((N, 8, 1, 1)) < 0.5, witness(rng, mu, ml), np.minimum((cs[..., ::-1][..., :V] * rng.random(mu.shape)).astype(np.int32), 255))
    th = bar(mu, ml, w, rng.choice(np.array([0, 1, CAP, 3 * CAP, V - 1]), (N, 8)))
    th = np.where(rng.random((N, 8)) < 0.2, rng.choice(np.array([0, 8160]), (N, 8)), th)
    return pack(x, w, th, up, lo, rl, snd)
def check_inputs(d):
    bad = []
    for k, least, most in (("x", 0, 255), ("w", 0, 255), ("th", 0, 8160), ("up", 0, W - 1), ("lo", 0, W - 1), ("rl", 0, W - 1), ("snd", 0, V - 1)):
        a = np.asarray(d[k]).astype(np.float64)
        if not (np.min(a) >= least and np.max(a) <= most): bad.append("range of " + k)
        elif np.any(a != np.floor(a)): bad.append("whole numbers in " + k)
    t = np.asarray(d["th"]).reshape(-1, 16)
    if np.any(t != t[:, :1]): bad.append("th alike in a group")
    return bad
def reference(x, w, th, up, lo, rl, snd):
    t = x.astype(np.float32).astype(np.int32).reshape(N, 8, 16, W).copy(); z = w.astype(np.float32).astype(np.int32).reshape(N, 8, 16, V)
    lim = th.astype(np.int64).reshape(N, 8, 16)[:, :, 0]
    hi = full(np.stack([gentries(a) for a in up])); dn = full(np.stack([gentries(a) for a in lo]))
    rh = rl.astype(np.int64).reshape(N, 8, 16, R).copy(); sl = np.stack([gentries(a) for a in snd]).astype(np.int64).reshape(N, 8, N - 1, G)
    last = np.zeros(N, np.int64)
    for rnd in range(RO):
        mu = reach(t, hi); ml = reach(t, dn)
        y = np.concatenate([mu[:, :, :8], ml[:, :, 8:]], axis=2)
        du = np.add.reduce(np.abs(mu[..., :V] - z), axis=2); dl = np.add.reduce(np.abs(ml[..., :V] - z), axis=2)
        bad = du + dl > lim[:, :, None] + (last & 15)[:, None, None]
        last = np.add.reduce(bad.reshape(N, 8 * V).astype(np.int64), axis=1)
        for a in range(N):
            for g in range(8):
                v = np.flatnonzero(bad[a, g])[:CAP]
                if len(v) == 0: continue
                upper = du[a, g, v] >= dl[a, g, v]
                h = np.where(upper, hi[a, g, v], dn[a, g, v]) & (R - 1)
                can = rh[a, g][:, h]
                e = np.add.reduce(np.abs(y[a, g][:, can] - z[a, g][:, v][:, None, :]), axis=0)
                k = np.argmin(e, axis=0); c = can[k, np.arange(len(v))]
                hi[a, g, v[upper]] = c[upper]; dn[a, g, v[~upper]] = c[~upper]
                cls, first = np.unique(h, return_index=True)
                rh[a, g, k[first], cls] = v[first]
        if rnd < RO - 1:
            for a in range(N):
                for d in range(1, N):
                    q = (a - d) % N
                    t[a, :, :, V + (d - 1) * G:V + d * G] = np.take_along_axis(y[q], sl[q, :, d - 1][:, None, :], 2)
    return {"y": np.ascontiguousarray(y[..., :V]).reshape(N, 128, V).astype(np.float32).astype(BF), "up1": np.stack([gtable(a) for a in hi[..., :V]]).astype(np.float32),
            "lo1": np.stack([gtable(a) for a in dn[..., :V]]).astype(np.float32), "rl1": rh.reshape(N, 128, R).astype(np.float32)}

@@ -1,0 +1,538 @@
+from concourse.bass import DstId, RemoteDMATransfer
+from concourse.mybir import AluOpType, ActivationFunctionType
+
+V, W, G, R, CAP, J, JP = 3136, 4096, 320, 1024, 256, 196, 208
+NV = 7
+TV = 96
+MAGIC = 201326592.0
+BF, F32, I32, U16 = "bfloat16", "float32", "int32", "uint16"
+SB = {
+    "x1": (W, BF), "x2": (W, BF), "au1": (W, BF), "au2": (W, BF), "bu": (W, BF), "al": (W, BF), "bl": (W, BF),
+    "qw": (W, BF), "q2u": (W, BF), "q2l": (W, BF), "q4": (V, BF), "ww": (V + 16, BF), "abu": (V, BF), "abl": (V, BF),
+    "cu": (V, BF), "cl": (V, BF),
+    "rli": (R, I32), "rlf": (R + CAP, F32), "iov": (V + 16, F32), "yc": (W, BF), "mx": (2048, BF), "abd": (2048, BF),
+    "si": (512, I32), "sf": (512, F32), "ya": (512, F32), "digb": (1024, BF), "q16": (512, U16), "pi16": (512, U16),
+    "p2u": (J, U16), "p2l": (J, U16), "p4u": (J, U16), "p4l": (J, U16),
+    "one": (144, BF), "idb": (128, BF), "idn": (128, BF), "id256": (128, BF), "id16": (128, BF), "m0": (128, BF),
+    "lm": (128, BF), "zz": (144, BF), "zu": (144, BF), "zl": (144, BF), "z0": (144, BF), "zr": (144, BF),
+    "m0f": (128, F32), "m0n": (128, F32), "idm": (128, F32), "onef": (128, F32),
+    "g16": (8, BF), "g32": (8, BF), "gn16": (8, BF), "kpat": (256, BF),
+    "pci": (8, I32), "col": (16, F32), "dd": (256, F32), "nm1": (256, F32), "nm2": (256, F32), "rs16": (256, BF),
+    "rsbig": (256, F32), "trow": (256, F32), "tw": (64, F32), "li": (32, I32), "l16": (32, U16),
+    "rs7": (NV * J, BF), "rs32": (512, BF), "c256": (J, BF), "ones": (256, BF),
+    "thi": (8, I32), "sni": (60, I32), "sn16": (60, U16), "sbuf": (3 * G, BF),
+    "thru": (J, F32), "dus": (J, F32), "bad": (J, BF), "ul": (2 * J, BF),
+    "ci": (JP, BF), "cmp": (NV * J, BF), "cms": (NV * J, BF), "junk": (16 * J, BF), "acc": (16, F32), "jf": (48, F32),
+    "key": (JP, F32), "ss": (JP, I32), "hh": (JP, I32), "j16": (16, U16), "h16": (16, U16), "v16": (16, U16),
+    "cj16": (16, U16), "of16": (16, U16), "ee": (256, BF), "zh": (256, F32), "zs": (256, F32), "hsc": (256, F32),
+    "hw": (16, F32), "ca16": (256, U16), "caf": (256, F32), "wv": (256, BF), "dv": (256, F32),
+    "xh": (256, F32), "eq": (512, BF), "eqs": (512, BF), "tiny": (64, F32), "pm": (256, F32), "pmx": (256, F32),
+    "oh": (256, BF), "zc": (256, F32), "zd": (256, F32), "ze": (256, F32), "pp": (264, F32), "gg": (JP, F32),
+    "po": (452, F32), "cnt": (8, F32),
+}
+SCRATCH = {k: ("sbuf", [128, n], d) for k, (n, d) in SB.items()}
+for _b in range(8):
+    SCRATCH["ps%d" % _b] = ("psum", [128, 512], F32)
+NDMA = 110
+SEMAPHORES = ["sv", "sa", "st", "sg", "arr", "sent"] + ["d%d" % _i for _i in range(NDMA)]
+SIZE = {BF: 2, F32: 4, I32: 4, U16: 2}
+A = AluOpType
+AF = ActivationFunctionType
+
+
+def rank_program(g, core, T, topo):
+    rank = T.rank_of(core)
+    if rank is None:
+        return
+    N = len(T.cores)
+    ops = []
+
+    def S(name, a=None, b=None, st=None, p=None):
+        n = 512 if name.startswith("ps") else SB[name][0]
+        a = 0 if a is None else a
+        b = n if b is None else b
+        sz = 4 if name.startswith("ps") else SIZE[SB[name][1]]
+        ps = slice(None) if p is None else p
+        ap = T[name][ps, a:b] if st is None else T[name][ps, a:b:st]
+        return (ap, [(name, a * sz, b * sz)])
+
+    def IX(win, off):
+        return (win[0].indirect(off[0]), win[1] + off[1], win[1], off[1])
+
+    def H(ap):
+        return (ap, [])
+
+    def val(x):
+        return x[0] if isinstance(x, tuple) else x
+
+    def add(q, fn, outs, ins, kind="c"):
+        rd, wr = [], []
+        for x in ins:
+            if isinstance(x, tuple):
+                rd += x[1]
+        for o in outs:
+            if len(o) == 4:
+                wr += o[2]
+                rd += o[3]
+            else:
+                wr += o[1]
+        ops.append((q, fn, rd, wr, kind))
+
+    def vcopy(o, i):
+        add("v", lambda: g.vector.tensor_copy(o[0], i[0]), [o], [i])
+
+    def vtt(o, a, b, op):
+        add("v", lambda: g.vector.tensor_tensor(o[0], a[0], b[0], op), [o], [a, b])
+
+    def vts(o, a, s1, op0, s2=None, op1=None):
+        if op1 is None:
+            add("v", lambda: g.vector.tensor_scalar(o[0], a[0], val(s1), None, op0), [o], [a, s1])
+        else:
+            add("v", lambda: g.vector.tensor_scalar(o[0], a[0], val(s1), val(s2), op0, op1), [o], [a, s1, s2])
+
+    def vscan(o, d0, d1, op0, op1):
+        add("v", lambda: g.vector.tensor_tensor_scan(o[0], d0[0], d1[0], 0.0, op0, op1), [o], [d0, d1])
+
+    def act(o, i, f, bias=0.0, scale=1.0, acc=None):
+        if acc is None:
+            add("a", lambda: g.scalar.activation(o[0], i[0], f, bias=val(bias), scale=val(scale)), [o], [i, bias, scale])
+        else:
+            add("a", lambda: g.scalar.activation(o[0], i[0], f, bias=val(bias), scale=val(scale), accum_out=acc[0]),
+                [o, acc], [i, bias, scale])
+
+    def mm(o, l, r, start=True, stop=True):
+        add("t", lambda: g.tensor.matmul(o[0], l[0], r[0], start, stop), [o], [l, r])
+
+    def iota(o, pat, base, ch):
+        if SB[o[1][0][0]][1] == I32:
+            add("g", lambda: g.iota(o[0], pat, base, ch), [o], [])
+        else:
+            add("g", lambda: g.iota(o[0], pat, base, ch, allow_small_or_imprecise_dtypes=True), [o], [])
+
+    def sel(o, i, pat, cmp, fill, base, ch):
+        add("g", lambda: g.affine_select(o[0], i[0], pat, cmp, fill, base, ch), [o], [i])
+
+    def dma(q, o, i):
+        eng = g.sync if q == "s" else g.scalar
+        add(q, lambda: eng.dma_start(o[0], i[0]), [o], [i], "d")
+
+    def wrap(o, z, src, a, n):
+        for r in range(16):
+            mm(o, S(z, 15 - r, 143 - r), S(src, a + r, a + 16 * n, 16), r == 0, r == 15)
+
+    def split(n):
+        act(S("ya", 0, n), S("sf", 0, n), AF.Identity, bias=-7.5)
+        act(S("ya", 0, n), S("ya", 0, n), AF.Identity, bias=MAGIC)
+        act(S("ps2", 0, n), S("ya", 0, n), AF.Identity, bias=-MAGIC)
+        act(S("digb", 0, n), S("ya", 0, n), AF.Identity, bias=-MAGIC)
+
+    def unwrap(n, whole, high):
+        vtt(S("digb", 512, 512 + n), high, whole, A.subtract)
+        dma("s", S("qw", p=slice(0, 128, 16)), S("digb", 0, 256))
+        dma("s", S("qw", p=slice(15, 128, 16)), S("digb", 256, 512))
+        dma("s", S("qw", p=slice(1, 128, 16)), S("digb", 512, 768))
+        dma("a", S("qw", p=slice(14, 128, 16)), S("digb", 768, 1024))
+        mm(S("ps4", 0, 452), S("id256"), S("digb", 512, 964), True, False)
+        mm(S("ps4", 0, 452), S("id16"), S("digb", 0, 452), False, True)
+
+    add("x", None, [S("x2", V, W)], [], "arr")
+
+    XCH = [(0, 24), (24, 56), (56, 98), (98, 146), (146, J)]
+    dma("s", S("si", 0, J), H(T.up[:, :]))
+    dma("a", S("si", 256, 256 + J), H(T.lo[:, :]))
+    dma("s", S("x1"), H(T.x[:, :]))
+    dma("s", S("x2", 0, 384), H(T.x[:, 0:384]))
+    add("v", lambda: g.vector.memset(T["qw"][:, :], 0.0), [S("qw")], [])
+    iota(S("pci", 0, 1), [[0, 1]], 0, 1)
+    iota(S("si", J, 256), [[16, 256 - J]], 16 * J, 1)
+    iota(S("one"), [[0, 144]], 1, 0)
+    sel(S("idb"), S("one", 0, 128), [[-1, 128]], A.is_equal, 0.0, 0, 1)
+    vts(S("pci", 4, 5), S("pci", 0, 1), 15, A.bitwise_and)
+    vtt(S("col", 1, 2), S("pci", 4, 5), S("pci", 0, 1), A.subtract)
+    vcopy(S("col", 0, 1), S("pci", 4, 5))
+    vts(S("col", 5, 6), S("col", 0, 1), -1.0, A.mult)
+    vts(S("col", 6, 7), S("col", 0, 1), -1.0, A.mult, 1.0, A.add)
+    vts(S("si", 256 + J, 512), S("si", J, 256), S("col", 1, 2), A.add)
+    vcopy(S("si", J, 256), S("si", 256 + J, 512))
+    act(S("id256"), S("idb"), AF.Identity, scale=-256.0)
+    act(S("id16"), S("idb"), AF.Identity, scale=0.0625)
+    vts(S("ya"), S("si"), -7.5, A.add, MAGIC, A.add)
+    vts(S("ps2"), S("ya"), -MAGIC, A.add)
+    act(S("digb", 0, 512), S("ya"), AF.Identity, bias=-MAGIC)
+    unwrap(512, S("si"), S("ps2"))
+    vcopy(S("q16", 0, 452), S("si", 0, 452))
+    vcopy(S("sf"), S("si"))
+    for a, b in XCH[1:]:
+        dma("s", S("x2", 16 * a, 16 * b), H(T.x[:, 16 * a:16 * b]))
+    iota(S("dd"), [[0, 16], [1, 16]], 0, 0)
+    iota(S("tw", 0, 16), [[16, 16]], 0, 0)
+    act(S("idn"), S("idb"), AF.Identity, scale=-1.0)
+    act(S("idm"), S("idb"), AF.Identity, scale=-8192.0)
+    act(S("nm1"), S("dd"), AF.Abs, bias=S("col", 5, 6))
+    act(S("nm2"), S("dd"), AF.Relu, bias=S("col", 6, 7))
+    act(S("tw", 0, 16), S("tw", 0, 16), AF.Identity, bias=S("col", 0, 1))
+    act(S("tw", 16, 32), S("tw", 0, 16), AF.Identity, bias=0.5)
+    act(S("tw", 32, 48), S("tw", 0, 16), AF.Identity, bias=float(R))
+    sel(S("zz"), S("one"), [[-16, 9], [0, 16]], A.is_ge, 0.0, 0, 1)
+    sel(S("m0"), S("zz", 0, 128), [[16, 8], [0, 16]], A.is_ge, 0.0, 15, -1)
+    sel(S("zz"), S("zz"), [[16, 9], [0, 16]], A.is_ge, 0.0, 15, -1)
+    sel(S("zz"), S("zz"), [[0, 9], [1, 16]], A.is_equal, 0.0, -15, 0)
+    vts(S("col", 2, 3), S("col", 0, 1), 1.0, A.is_le)
+    vts(S("col", 3, 4), S("col", 0, 1), 14.0, A.is_ge)
+    vts(S("col", 10, 11), S("col", 0, 1), -2.0, A.mult, 1.0, A.add)
+    vts(S("col", 11, 12), S("col", 0, 1), 2.0, A.mult, -29.0, A.add)
+    vtt(S("col", 2, 4), S("col", 2, 4), S("col", 10, 12), A.mult)
+    vts(S("col", 4, 5), S("col", 0, 1), 0.0, A.is_le)
+    vcopy(S("pi16", 0, 452), S("ps4", 0, 452))
+    act(S("zu"), S("zz"), AF.Identity, scale=S("col", 2, 3))
+    act(S("zl"), S("zz"), AF.Identity, scale=S("col", 3, 4))
+    act(S("z0"), S("zz"), AF.Identity, scale=S("col", 4, 5))
+    act(S("zr"), S("zz"), AF.Identity, scale=S("col", 0, 1))
+
+    def late_loads():
+        dma("s", S("thi", 0, 1), H(T.th[:, :]))
+        dma("s", S("sni"), H(T.snd[:, :]))
+        dma("s", S("au1", V, W), H(T.x[:, V:W]))
+        iota(S("q2u", V, W), [[16, 60], [0, 16]], V, 0)
+        iota(S("q2l", V, W), [[0, 60], [-1, 16]], 0, 0)
+        iota(S("ones"), [[0, 256]], 1, 0)
+        sel(S("lm"), S("m0"), [[1, 128]], A.is_gt, 0.0, 0, -1)
+        sel(S("lm"), S("lm"), [[1, 128]], A.not_equal, -512.0, 0, -1)
+        sel(S("m0f"), S("m0"), [[0, 128]], A.is_ge, 0.0, 0, 0)
+        iota(S("onef"), [[0, 128]], 1, 0)
+        for nm, c in (("m0n", -1), ("g16", 16), ("g32", 32), ("gn16", -16)):
+            n = SB[nm][0]
+            iota(S(nm), [[0, n]], c, 0)
+            sel(S(nm), S(nm), [[-16, 8], [0, n // 8]], A.is_ge, 0.0, 0, 1)
+            sel(S(nm), S(nm), [[16, 8], [0, n // 8]], A.is_ge, 0.0, 15, -1)
+        iota(S("kpat"), [[0, 16], [1, 16]], 0, 0)
+        sel(S("rs16"), S("ones"), [[0, 16], [1, 16]], A.is_gt, 0.0, 0, 0)
+        sel(S("rsbig"), S("rs16"), [[0, 16], [1, 16]], A.is_gt, 1048576.0, 0, 0)
+        sel(S("rsbig"), S("rsbig"), [[0, 16], [1, 16]], A.is_equal, 0.0, 0, 0)
+        iota(S("trow"), [[1, 256]], -512, 0)
+        iota(S("li", 0, 16), [[16, 16]], 15, 0)
+        iota(S("li", 16, 32), [[1, 16]], 0, 0)
+        iota(S("rs7"), [[0, NV * J]], 1, 0)
+        sel(S("rs7"), S("rs7"), [[0, NV], [1, J]], A.is_gt, 0.0, 0, 0)
+        iota(S("rs32"), [[0, 512]], 1, 0)
+        sel(S("rs32"), S("rs32"), [[0, 16], [1, 32]], A.is_gt, 0.0, 0, 0)
+        iota(S("c256"), [[0, J]], 256, 0)
+        for nm, a, b in (("ci", 0, JP), ("key", J, JP), ("ss", J, JP), ("hh", J, JP), ("eq", 0, 32), ("pp", 0, 264),
+                         ("ww", V, V + 16), ("rlf", R, R + CAP)):
+            iota(S(nm, a, b), [[0, b - a]], 0, 0)
+        iota(S("iov"), [[1, V + 16]], 0, 0)
+
+    def later_loads():
+        dma("s", S("q2u", V, W, p=slice(1, 128, 16)), S("q2l", V, W, p=slice(1, 128, 16)))
+        dma("s", S("q2l", V, W, p=slice(15, 128, 16)), S("q2u", V, W, p=slice(15, 128, 16)))
+        dma("s", S("al", V, W), H(T.x[:, V:W]))
+
+    PCH = [(0, 66), (66, 132), (132, J)]
+    UCH = [(0, 64), (64, 128), (128, J)]
+    LCH = [(0, 64), (64, 128), (128, 176), (176, J)]
+    bank = [0]
+
+    def level(o, src, own, lst, base, a, b, copy=None):
+        vtt(S(o, 16 * a, 16 * b), IX(S(src), S(lst, base + a, base + b)), S(own, 16 * a, 16 * b), A.max)
+        if copy:
+            dma("s", S(copy, 16 * a, 16 * b), S(o, 16 * a, 16 * b))
+
+    def levels(o, src, own, lst, base, copy):
+        for a, b in ((0, 98), (98, J)):
+            level(o, src, own, lst, base, a, b, copy)
+
+    def chase(o, src, lst, base, z, ps, between=None):
+        for a, b in PCH:
+            act(S(o, 16 * a, 16 * b), IX(S(src), S(lst, base + a, base + b)), AF.Identity)
+            if between and b == J:
+                between()
+            wrap(S(ps, a, b), z, o, 16 * a, b - a)
+
+    def distance(m, ab, a, b):
+        n = (b - a + 31) // 32
+        cut = [a + (b - a) * i // n for i in range(n + 1)]
+        for i in range(n):
+            c0, c1 = 16 * cut[i], 16 * cut[i + 1]
+            pb = S("ps%d" % (bank[0] % 3), 0, c1 - c0)
+            bank[0] += 1
+            mm(pb, S("idn"), S("ww", c0, c1), True, False)
+            mm(pb, S("idb"), S(m, c0, c1), False, True)
+            act(S(ab, c0, c1), pb, AF.Abs)
+
+    def merge(au, a, b):
+        for k in range(8):
+            rows = slice(16 * k + 8, 16 * k + 16)
+            dma("s", S(au, a, b, p=rows), S("al", a, b, p=rows))
+
+    def rhyme_write():
+        for q in range(7, -1, -1):
+            vtt(IX(S("rlf"), S("of16", 2 * q, 2 * q + 2)), S("zd", 32 * q, 32 * q + 32), S("caf", 32 * q, 32 * q + 32), A.add)
+
+    def pointers(o):
+        vtt(S("ze"), S("ps1", 0, 256), S("ee"), A.mult)
+        vscan(S("pp", 1, 257), S("ones"), S("ze"), A.mult, A.add)
+        vcopy(S("gg"), IX(S("pp"), S("cj16", 0, 13)))
+        vtt(S("ps2", 0, J), S("gg", 1, J + 1), S("gg", 0, J), A.subtract)
+        vtt(S("ps3", 0, J), S("ps2", 0, J), S("ul", 0, J), A.mult)
+        vtt(S("ps3", 256, 452), S("ps2", 0, J), S("ul", J, 2 * J), A.mult)
+        vtt(S(o, 0, J), S("ps3", 0, J), S("sf", 0, J), A.add)
+        vtt(S(o, 256, 452), S("ps3", 256, 452), S("sf", 256, 452), A.add)
+
+    for rnd in range(2):
+        xs, xo, au = ("x1", "x2", "au1") if rnd == 0 else ("x2", "x1", "au2")
+        thr = S("col", 8 + rnd, 9 + rnd)
+        if rnd == 0:
+            late_loads()
+            for a, b in XCH[:3]:
+                level(au, xs, xo, "q16", 0, a, b)
+        else:
+            split(452)
+            vcopy(S("q16", 0, 452), S("sf", 0, 452))
+            level(au, xs, xo, "q16", 0, 0, 40)
+            unwrap(452, S("sf", 0, 452), S("ps2", 0, 452))
+            level(au, xs, xo, "q16", 0, 40, 60)
+            vcopy(S("pi16", 0, 452), S("ps4", 0, 452))
+            level(au, xs, xo, "q16", 0, 60, 98)
+        dma("s", S("cu", 0, 1568), S(au, 0, 1568))
+        level(au, xs, xo, "q16", 0, 98, 146)
+        level(au, xs, xo, "q16", 0, 146, J)
+        dma("s", S("cu", 1568, V), S(au, 1568, V))
+        if rnd == 0:
+            later_loads()
+        chase("q2u", "qw", "pi16", 0, "zu", "ps3")
+        levels("al", xs, xo, "q16", 256, "cl")
+        vcopy(S("p2u"), S("ps3", 0, J))
+        chase("q2l", "qw", "pi16", 256, "zl", "ps4")
+        if rnd == 0:
+            dma("s", S("bu", V, W), H(T.x[:, V:W]))
+            dma("s", S("ww", 0, V), H(T.w[:, :]))
+        levels("bu", au, "cu", "p2u", 0, "cu")
+        if rnd == 0:
+            dma("s", S("bl", V, W), H(T.x[:, V:W]))
+        vcopy(S("p2l"), S("ps4", 0, J))
+        chase("q4", "q2u", "p2u", 0, "zu", "ps3")
+        levels("bl", "al", "cl", "p2l", 0, "cl")
+        vcopy(S("p4u"), S("ps3", 0, J))
+        if rnd == 0:
+            dma("s", S("rli"), H(T.rl[:, :]))
+            vcopy(thr, S("thi", 0, 1))
+        for a, b in UCH:
+            level(au, "bu", "cu", "p4u", 0, a, b)
+        chase("q4", "q2l", "p2l", 0, "zl", "ps4", lambda au=au: distance(au, "abu", 0, 64))
+        vcopy(S("p4l"), S("ps4", 0, J))
+        distance(au, "abu", 64, 128)
+        wrap(S("ps5", 0, 64), "zz", "abu", 0, 64)
+        distance(au, "abu", 128, J)
+        wrap(S("ps5", 64, 128), "zz", "abu", 1024, 64)
+        for i, (a, b) in enumerate(LCH):
+            level("al", "bl", "cl", "p4l", 0, a, b)
+            distance("al", "abl", a, b)
+            if i == 0:
+                wrap(S("ps5", 128, J), "zz", "abu", 2048, J - 128)
+            if i == 1:
+                act(S("thru"), S("ps5", 0, J), AF.Identity, bias=thr, scale=-1.0)
+                act(S("dus"), S("ps5", 0, J), AF.Identity)
+                merge(au, 0, 2048)
+                wrap(S("ps6", 0, 64), "zz", "abl", 0, 64)
+        wrap(S("ps6", 64, 128), "zz", "abl", 1024, 64)
+        wrap(S("ps6", 128, J), "zz", "abl", 2048, J - 128)
+        merge(au, 2048, V)
+        mm(S("ps1", 0, 256), S("idm"), S("nm1"), True, False)
+        vtt(S("ps7", 0, J), S("sf", 0, J), S("sf", 256, 256 + J), A.subtract)
+        if rnd == 0:
+            vcopy(S("rlf", 0, R), S("rli"))
+            vcopy(S("sn16"), S("sni"))
+            vcopy(S("l16"), S("li"))
+        else:
+            rhyme_write()
+            dma("s", H(T.y[:, :]), S(au, 0, V))
+        vtt(S("bad"), S("ps6", 0, J), S("thru"), A.is_gt)
+        mm(S("ps3", 0, J), S("m0"), S("bad"))
+        mm(S("ps4", 0, J), S("lm"), S("bad"))
+        vtt(S("ul", 0, J), S("ps6", 0, J), S("dus"), A.is_le)
+        vscan(S("ci", 1, J + 1), S("ps3", 0, J), S("c256"), A.add, A.min)
+        for a in range(NV, 16):
+            act(S("junk", a * J, a * J + J), S("ci", 1, J + 1), AF.Sign, bias=S("tw", 16 + a, 17 + a), scale=-1.0,
+                acc=S("acc", a, a + 1))
+        vtt(S("ps7", 256, 256 + J), S("ps7", 0, J), S("ul", 0, J), A.mult)
+        for a in range(NV):
+            vts(S("cmp", a * J, a * J + J), S("ci", 1, J + 1), S("tw", a, a + 1), A.is_le)
+        wrap(S("ps5", 0, 13), "z0", "ci", 0, 13)
+        vtt(S("ss", 0, J), S("ps7", 256, 256 + J), S("sf", 256, 256 + J), A.add)
+        vscan(S("cms"), S("rs7"), S("cmp"), A.mult, A.add)
+        vtt(S("key", 0, J), S("ps4", 0, J), S("ci", 0, J), A.add)
+        vcopy(S("jf", 0, NV), S("cms", J - 1, NV * J, J))
+        act(S("jf", NV, 16), S("acc", NV, 16), AF.Identity, bias=J / 2.0, scale=0.5)
+        vts(S("hh", 0, J), S("ss", 0, J), R - 1, A.bitwise_and)
+        vcopy(S("j16"), S("jf", 0, 16))
+        act(S("jf", 16, 32), S("jf", 0, 16), AF.Identity, scale=16.0)
+        if rnd == 0:
+            act(S("sbuf"), IX(S(au), S("sn16")), AF.Identity)
+            far = [d for d in range(1, N) if topo.chip(T.cores[(rank + d) % N]) != topo.chip(core)]
+            out = topo.engines(core, T.cores[(rank + far[0]) % N])
+            per = len(out) // len(far)
+            eng = {d: out[per * i:per * i + per] for i, d in enumerate(far)}
+            for d in range(1, N):
+                if d not in far:
+                    eng[d] = [e for e in topo.engines(core, T.cores[(rank + d) % N]) if e not in out]
+            total = sum(len(eng[d]) for d in eng)
+            trs = []
+            for d in range(1, N):
+                rid, pid, _ = topo.addr(T.cores[(rank + d) % N])
+                trs.append(RemoteDMATransfer(dst_ids=[DstId(rid=rid, pnc=pid)], dma_engine_mask=sum(1 << e for e in eng[d]),
+                                             remote_sem=T.sem.arr, src=T["sbuf"][:, (d - 1) * G:d * G],
+                                             dst=T["x2"][:, V + (d - 1) * G:V + d * G]))
+            add("g", lambda trs=trs: g.remote_dma_fused(trs, local_sem=T.sem.sent), [], [S("sbuf")], "r")
+            for b in ("au2", "al", "bu", "bl"):
+                dma("s", S(b, V, W), S("x2", V, W))
+        vtt(S("ee"), IX(S("key"), S("j16")), S("trow"), A.is_equal)
+        vtt(S("zh"), IX(S("hh"), S("j16")), S("ee"), A.mult)
+        wrap(S("ps0", 0, 16), "zr", "ee", 0, 16)
+        mm(S("ps1", 0, 256), S("m0f"), S("zh"), False, True)
+        vtt(S("jf", 32, 48), S("ps0", 0, 16), S("jf", 16, 32), A.add)
+        vcopy(S("v16"), S("jf", 32, 48))
+        act(S("wv"), IX(S("ww"), S("v16")), AF.Identity)
+        vscan(S("hsc"), S("rs16"), S("ps1", 0, 256), A.mult, A.max)
+        vcopy(S("h16"), S("hsc", 15, 256, 16))
+        act(S("hw"), S("hsc", 15, 256, 16), AF.Identity)
+        mm(S("ps6", 0, 128), S("idb"), S("wv", 0, 128))
+        mm(S("ps4", 0, 256), S("idb"), S("kpat"), True, False)
+        vcopy(S("ca16"), IX(S("rlf"), S("h16")))
+        act(S("xh"), IX(S("hw"), S("l16", 16, 32)), AF.Identity)
+        mm(S("ps7", 0, 256), S("m0f"), S("zh"))
+        mm(S("ps7", 256, 512), S("idm"), S("nm2"), True, False)
+        mm(S("ps7", 256, 512), S("m0f"), S("zh"), False, True)
+        vcopy(S("yc", 0, 16 * TV), IX(S(au), S("ca16", 0, TV)))
+        for c in range(2):
+            t0 = TV if c == 0 else 192
+            act(S("yc", 16 * t0, 3072 + 1024 * c), IX(S(au), S("ca16", t0, 192 + 64 * c)), AF.Identity)
+            for k in range(16):
+                o = S("ps%d" % (k // 4), 128 * (k % 4) + 64 * c, 128 * (k % 4) + 64 * c + 64)
+                mm(o, S("idn"), S("wv", 128 + 64 * c, 192 + 64 * c), True, False)
+                mm(o, S("idb"), S("yc", 2048 + 1024 * c + k, 3072 + 1024 * c, 16), False, True)
+            if c == 0:
+                for k in range(16):
+                    mm(S("ps4", k, 128, 16), S("yc", k, 2048, 16), S("gn16"), False, False)
+        vcopy(S("cj16", 0, 13), S("ps5", 0, 13))
+        vtt(S("eq", 0, 512, 2), S("ps7", 256, 512), S("xh"), A.is_equal)
+        vtt(S("eq", 33, 512, 2), S("ps7", 0, 240), S("xh", 16, 256), A.is_equal)
+        vtt(S("zs"), IX(S("ss"), S("j16")), S("ee"), A.mult)
+        vscan(S("eqs"), S("rs32"), S("eq"), A.mult, A.add)
+        vts(S("tiny", 0, 16), S("tw", 0, 16), S("ci", J, J + 1), A.is_lt)
+        for b in range(4):
+            act(S("abd", 512 * b, 512 * b + 512), S("ps%d" % b), AF.Abs)
+            for k in range(4 * b, 4 * b + 4):
+                vtt(S("mx", 128 * k, 128 * k + 128), S("ps6", 0, 128), S("yc", k, 2048, 16), A.max)
+            if b == 0:
+                vtt(S("tiny", 16, 32), S("eqs", 31, 512, 32), S("tiny", 0, 16), A.is_ge)
+            if b == 1:
+                vtt(S("tiny", 32, 48), S("tiny", 16, 32), S("tw", 32, 48), A.mult)
+            if b == 2:
+                vtt(S("tiny", 48, 64), S("tiny", 32, 48), S("hw"), A.max)
+            if b == 3:
+                vcopy(S("of16"), S("tiny", 48, 64))
+            for k in range(4 * b, 4 * b + 4):
+                mm(S("ps4", k, 128, 16), S("mx", 128 * k, 128 * k + 128), S("g32"), False, False)
+            for k in range(4 * b, 4 * b + 4):
+                mm(S("ps4", 128 + k, 256, 16), S("abd", 128 * k, 128 * k + 128), S("g16"), False, k == 15)
+        act(S("caf"), IX(S("rlf"), S("h16")), AF.Identity)
+        act(S("ul", J, 2 * J), S("ul", 0, J), AF.Identity, bias=1.0, scale=-1.0)
+        vscan(S("pm"), S("rsbig"), S("ps4", 0, 256), A.add, A.min)
+        mm(S("ps1", 0, 256), S("m0n"), S("zs"), True, False)
+        if rnd == 0:
+            act(S("junk", 0, J), S("bad"), AF.Identity, acc=S("cnt", 0, 1))
+        vcopy(S("pmx"), IX(S("pm"), S("l16", 0, 16)))
+        vtt(S("oh"), S("ps4", 0, 256), S("pmx"), A.is_equal)
+        for h in range(2):
+            mm(S("ps6", 128 * h, 128 * h + 128), S("oh", 128 * h, 128 * h + 128), S("idb"))
+        vtt(S("dv"), IX(S("iov"), S("v16")), S("caf"), A.subtract)
+        vtt(S("zc"), S("ps6", 0, 256), S("caf"), A.mult)
+        mm(S("ps1", 0, 256), S("m0f"), S("zc"), False, True)
+        vtt(S("zd"), S("ps6", 0, 256), S("dv"), A.mult)
+        if rnd == 0:
+            mm(S("ps5", 100, 101), S("onef"), S("cnt", 0, 1))
+            act(S("cnt", 1, 2), S("ps5", 100, 101), AF.Identity, bias=-7.5)
+            act(S("cnt", 2, 3), S("cnt", 1, 2), AF.Identity, bias=MAGIC)
+            act(S("cnt", 3, 4), S("cnt", 2, 3), AF.Identity, bias=MAGIC, scale=-1.0)
+            act(S("cnt", 4, 5), S("ps5", 100, 101), AF.Identity, bias=S("cnt", 3, 4))
+            act(S("col", 9, 10), S("cnt", 4, 5), AF.Identity, bias=S("col", 8, 9))
+            pointers("sf")
+        else:
+            rhyme_write()
+            dma("s", H(T.rl1[:, 0:512]), S("rlf", 0, 512))
+            dma("a", H(T.rl1[:, 512:R]), S("rlf", 512, R))
+            pointers("po")
+            dma("s", H(T.up1[:, :]), S("po", 0, J))
+            dma("a", H(T.lo1[:, :]), S("po", 256, 452))
+
+    emit(g, T, ops, total)
+
+
+def emit(g, T, ops, total):
+    queue = {"v": g.vector, "a": g.scalar, "t": g.tensor, "g": g, "s": g.sync}
+    csem = {"v": T.sem.sv, "a": T.sem.sa, "t": T.sem.st, "g": T.sem.sg}
+    src = [o[0] if o[4] == "c" else i for i, o in enumerate(ops)]
+    seen, known, clock, waits = {}, {q: {} for q in queue}, [None] * len(ops), [[] for _ in ops]
+    for i, (q, fn, rd, wr, kind) in enumerate(ops):
+        need = {}
+        for regions, w in ((rd, False), (wr, True)):
+            for name, a, b in regions:
+                psum = name.startswith("ps")
+                for j, w2, a2, b2 in seen.get(name, []):
+                    same = ops[j][4] == "c" and kind == "c" and ops[j][0] == q
+                    if psum and not same:
+                        hit = True
+                    elif same and q == "t":
+                        hit = False
+                    elif w and w2 and (kind == "c") != (ops[j][4] == "c"):
+                        hit = a // 16 < -(-b2 // 16) and a2 // 16 < -(-b // 16)
+                    elif w and w2 and kind == "d" and ops[j][4] == "d" and name in ("qw", "au1", "au2") and rd \
+                            and ops[j][2] and ops[j][2][0][0] == rd[0][0]:
+                        hit = False
+                    else:
+                        hit = (w or w2) and a < b2 and a2 < b
+                    if hit and need.get(src[j], -1) < j:
+                        need[src[j]] = j
+        for regions, w in ((rd, False), (wr, True)):
+            for name, a, b in regions:
+                seen.setdefault(name, []).append((i, w, a, b))
+        if kind == "arr":
+            clock[i] = {i: i}
+            continue
+        kn = known[q]
+        for j in sorted(need.values(), reverse=True):
+            if kn.get(src[j], -1) >= j:
+                continue
+            waits[i].append(j)
+            for s, k in clock[j].items():
+                if kn.get(s, -1) < k:
+                    kn[s] = k
+        clock[i] = dict(kn)
+        clock[i][src[i]] = i
+    last = {}
+    for i, o in enumerate(ops):
+        if o[4] == "c":
+            last[o[0]] = i
+    used = set(j for ws in waits for j in ws) | set(last.values())
+    token, count, nd = {}, {q: 0 for q in csem}, 0
+    for i, (q, fn, rd, wr, kind) in enumerate(ops):
+        if kind == "arr":
+            token[i] = (T.sem.arr, total)
+            continue
+        for j in waits[i]:
+            queue[q].wait_ge(token[j][0], token[j][1])
+        ins = fn()
+        if kind == "d":
+            token[i] = (T.sem["d%d" % nd], 16)
+            nd += 1
+            ins.then_inc(token[i][0], 16)
+        elif kind == "r":
+            token[i] = (T.sem.sent, total)
+        elif i in used:
+            count[q] += 1
+            token[i] = (csem[q], count[q])
+            ins.then_inc(csem[q], 1)
+    done = set(j for ws in waits for j in ws)
+    for i, o in enumerate(ops):
+        if (o[4] != "c" and i not in done) or (o[4] == "c" and last[o[0]] == i):
+            g.sync.wait_ge(token[i][0], token[i][1])

@@ -1,43 +1,57 @@
 from concourse.bass import DstId, RemoteDMATransfer
 from concourse.mybir import AluOpType, ActivationFunctionType
 
-V, W, G, R, CAP, J, JP = 3136, 4096, 320, 1024, 256, 196, 208
-NV = 7
-TV = 96
+V, W, G, R, CAP, J, JP, JW = 3136, 4096, 320, 1024, 256, 196, 208, 224
+TE = 32
+UNIT = 4096.0
 MAGIC = 201326592.0
-BF, F32, I32, U16 = "bfloat16", "float32", "int32", "uint16"
+SH = 16384
+BF, F32, I32, U16, F16 = "bfloat16", "float32", "int32", "uint16", "float16"
 SB = {
     "x1": (W, BF), "x2": (W, BF), "au1": (W, BF), "au2": (W, BF), "bu": (W, BF), "al": (W, BF), "bl": (W, BF),
-    "qw": (W, BF), "q2u": (W, BF), "q2l": (W, BF), "q4": (V, BF), "ww": (V + 16, BF), "abu": (V, BF), "abl": (V, BF),
-    "cu": (V, BF), "cl": (V, BF),
-    "rli": (R, I32), "rlf": (R + CAP, F32), "iov": (V + 16, F32), "yc": (W, BF), "mx": (2048, BF), "abd": (2048, BF),
-    "si": (512, I32), "sf": (512, F32), "ya": (512, F32), "digb": (1024, BF), "q16": (512, U16), "pi16": (512, U16),
+    "qw": (W, BF), "qn": (2 * W + CAP, BF), "pcj": (J, I32), "pc16": (J, U16), "sf": (512, F32), "q2u": (W, BF), "q2l": (W, BF), "q4": (V, BF), "ww": (V + 16, BF), "abu": (V, BF), "abl": (V, BF),
+    "cu": (V, BF), "cl": (V, BF), "pt": (2 * V + CAP, F32),
+    "rli": (R, I32), "rlf": (R + CAP, F32), "yc": (W, BF), "mx": (2048, BF), "abd": (2048, BF),
+    "si": (512, I32), "ya": (512, F32), "digb": (1024, BF), "idq": (128, BF), "idqn": (128, BF), "crb": (256, BF),
+    "q16": (512, U16), "pi16": (512, U16), "eb": (512, BF),
     "p2u": (J, U16), "p2l": (J, U16), "p4u": (J, U16), "p4l": (J, U16),
-    "one": (144, BF), "idb": (128, BF), "idn": (128, BF), "id256": (128, BF), "id16": (128, BF), "m0": (128, BF),
-    "lm": (128, BF), "zz": (144, BF), "zu": (144, BF), "zl": (144, BF), "z0": (144, BF), "zr": (144, BF),
-    "m0f": (128, F32), "m0n": (128, F32), "idm": (128, F32), "onef": (128, F32),
-    "g16": (8, BF), "g32": (8, BF), "gn16": (8, BF), "kpat": (256, BF),
-    "pci": (8, I32), "col": (16, F32), "dd": (256, F32), "nm1": (256, F32), "nm2": (256, F32), "rs16": (256, BF),
-    "rsbig": (256, F32), "trow": (256, F32), "tw": (64, F32), "li": (32, I32), "l16": (32, U16),
-    "rs7": (NV * J, BF), "rs32": (512, BF), "c256": (J, BF), "ones": (256, BF),
+    "one": (144, BF), "idb": (128, BF), "idn": (128, BF), "id256": (128, BF), "id16": (128, BF),
+    "m0": (128, BF), "lm": (128, BF), "m16": (128, BF), "mr": (128, BF), "lb1": (128, BF),
+    "idk": (128, F32), "idkn": (128, F32), "la": (128, F32), "thru": (J, F32), "dus": (J, F32),
+    "zz": (144, BF), "zu1": (144, BF), "zu3": (144, BF), "zr": (144, BF), "big": (1, BF),
+    "g16": (8, BF), "g32": (8, BF), "gn16": (8, BF), "kpat": (256, BF), "zero": (128, BF), "n64": (256, BF),
+    "pci": (8, I32), "col": (16, F32), "dd": (256, F32), "nm": (256, BF), "rsbig": (256, F32), "trow": (256, BF),
+    "trm": (256, BF), "dump": (64, F32), "li": (16, I32), "l16": (16, U16), "gi": (64, I32),
     "thi": (8, I32), "sni": (60, I32), "sn16": (60, U16), "sbuf": (3 * G, BF),
-    "thru": (J, F32), "dus": (J, F32), "bad": (J, BF), "ul": (2 * J, BF),
-    "ci": (JP, BF), "cmp": (NV * J, BF), "cms": (NV * J, BF), "junk": (16 * J, BF), "acc": (16, F32), "jf": (48, F32),
-    "key": (JP, F32), "ss": (JP, I32), "hh": (JP, I32), "j16": (16, U16), "h16": (16, U16), "v16": (16, U16),
-    "cj16": (16, U16), "of16": (16, U16), "ee": (256, BF), "zh": (256, F32), "zs": (256, F32), "hsc": (256, F32),
-    "hw": (16, F32), "ca16": (256, U16), "caf": (256, F32), "wv": (256, BF), "dv": (256, F32),
-    "xh": (256, F32), "eq": (512, BF), "eqs": (512, BF), "tiny": (64, F32), "pm": (256, F32), "pmx": (256, F32),
-    "oh": (256, BF), "zc": (256, F32), "zd": (256, F32), "ze": (256, F32), "pp": (264, F32), "gg": (JP, F32),
-    "po": (452, F32), "cnt": (8, F32),
+    "bad": (JP, BF), "sc": (JW, BF), "ul": (JW, BF), "key": (JW, F32), "hh": (JW, F32), "ra": (J, F32),
+    "bw": (JW, F32), "cm1": (256, BF), "cm2": (256, BF), "ee": (256, BF), "zh": (256, F16),
+    "a16": (16, U16), "j16": (16, U16), "h16": (16, U16), "v16": (16, U16), "of16": (32, U16),
+    "tiny": (96, F32), "val": (16, BF), "tj": (256, BF), "te": (256, BF), "xh": (256, F32), "eq": (512, BF),
+    "ca16": (256, U16), "caf": (256, F32), "cah": (256, F16), "wv": (256, BF), "dv": (256, F32),
+    "pm": (256, F32), "pmx": (256, F32), "oh": (256, BF), "zc": (256, F32), "zch": (256, F16), "zd": (256, F32),
+    "crow": (256, F32), "cnt": (8, F32),
 }
 SCRATCH = {k: ("sbuf", [128, n], d) for k, (n, d) in SB.items()}
-for _b in range(8):
+PSUM = {"ps0": ("psa", 0), "ps1": ("psa", 512), "ps2": ("psb", 0), "ps3": ("psb", 512)}
+SCRATCH["psa"] = ("psum", [128, 1024], F32)
+SCRATCH["psb"] = ("psum", [128, 1024], F32)
+for _b in range(4, 8):
     SCRATCH["ps%d" % _b] = ("psum", [128, 512], F32)
-NDMA = 110
+    PSUM["ps%d" % _b] = ("ps%d" % _b, 0)
+NDMA = 120
 SEMAPHORES = ["sv", "sa", "st", "sg", "arr", "sent"] + ["d%d" % _i for _i in range(NDMA)]
-SIZE = {BF: 2, F32: 4, I32: 4, U16: 2}
+SIZE = {BF: 2, F32: 4, I32: 4, U16: 2, F16: 2}
+ALL = (1 << 128) - 1
 A = AluOpType
 AF = ActivationFunctionType
+XCH = [(0, 48), (48, 72), (72, 98), (98, 146), (146, J)]
+HALF = [(0, 98), (98, J)]
+FIRST = [(0, 64), (64, J)]
+NAT = [(0, 56), (56, 96), (96, 148), (148, J)]
+THIRD = [(0, 64), (64, 128), (128, J)]
+LCH = [(a, a + 32) for a in range(0, 160, 32)] + [(160, 180), (180, J)]
+LSUM = [(2, 0, 64), (6, 64, 128), (6, 128, J)]
+LMERGE = [(3, 0, 128), (6, 128, J)]
 
 
 def rank_program(g, core, T, topo):
@@ -48,13 +62,23 @@ def rank_program(g, core, T, topo):
     ops = []
 
     def S(name, a=None, b=None, st=None, p=None):
-        n = 512 if name.startswith("ps") else SB[name][0]
+        nm, o = PSUM.get(name, (name, 0))
+        n, sz = (512, 4) if name in PSUM else (SB[name][0], SIZE[SB[name][1]])
         a = 0 if a is None else a
         b = n if b is None else b
-        sz = 4 if name.startswith("ps") else SIZE[SB[name][1]]
         ps = slice(None) if p is None else p
-        ap = T[name][ps, a:b] if st is None else T[name][ps, a:b:st]
-        return (ap, [(name, a * sz, b * sz)])
+        mask = ALL if p is None else sum(1 << i for i in range(128)[p])
+        ap = T[nm][ps, o + a:o + b] if st is None else T[nm][ps, o + a:o + b:st]
+        return (ap, [(name, a * sz, b * sz, mask)])
+
+    def P2(i, n):
+        return (T["psa" if i == 0 else "psb"][:, 0:n], [("ps%d" % (2 * i + k), 0, 2048, ALL) for k in range(-(-n // 512))])
+
+    def REV(name):
+        return (T[name][:, ::-1], S(name)[1])
+
+    def ROW(name, r, a, b):
+        return S(name, a, b, p=slice(r, 128, 16))
 
     def IX(win, off):
         return (win[0].indirect(off[0]), win[1] + off[1], win[1], off[1])
@@ -93,377 +117,495 @@ def rank_program(g, core, T, topo):
     def vscan(o, d0, d1, op0, op1):
         add("v", lambda: g.vector.tensor_tensor_scan(o[0], d0[0], d1[0], 0.0, op0, op1), [o], [d0, d1])
 
-    def act(o, i, f, bias=0.0, scale=1.0, acc=None):
-        if acc is None:
-            add("a", lambda: g.scalar.activation(o[0], i[0], f, bias=val(bias), scale=val(scale)), [o], [i, bias, scale])
-        else:
-            add("a", lambda: g.scalar.activation(o[0], i[0], f, bias=val(bias), scale=val(scale), accum_out=acc[0]),
-                [o, acc], [i, bias, scale])
+    def act(o, i, f=AF.Identity, bias=0.0, scale=1.0):
+        add("a", lambda: g.scalar.activation(o[0], i[0], f, bias=val(bias), scale=val(scale)), [o], [i, bias, scale])
 
     def mm(o, l, r, start=True, stop=True):
         add("t", lambda: g.tensor.matmul(o[0], l[0], r[0], start, stop), [o], [l, r])
 
-    def iota(o, pat, base, ch):
+    def iota(o, pat, base, ch=0):
         if SB[o[1][0][0]][1] == I32:
             add("g", lambda: g.iota(o[0], pat, base, ch), [o], [])
         else:
             add("g", lambda: g.iota(o[0], pat, base, ch, allow_small_or_imprecise_dtypes=True), [o], [])
 
-    def sel(o, i, pat, cmp, fill, base, ch):
-        add("g", lambda: g.affine_select(o[0], i[0], pat, cmp, fill, base, ch), [o], [i])
+    def fill(o, c):
+        iota(o, [[0, o[0].shape[1]]], c)
 
-    def dma(q, o, i):
-        eng = g.sync if q == "s" else g.scalar
-        add(q, lambda: eng.dma_start(o[0], i[0]), [o], [i], "d")
+    def sel(o, i, pat, cmp, fl, base, ch):
+        add("g", lambda: g.affine_select(o[0], i[0], pat, cmp, fl, base, ch), [o], [i])
 
-    def wrap(o, z, src, a, n):
+    def rows(o, i, lo, hi):
+        n = o[0].shape[1]
+        nb, wd = (8, 1) if n == 8 else (n // 16, 16)
+        sel(o, i, [[-16, nb], [0, wd]], A.is_ge, 0.0, -lo, 1)
+        sel(o, o, [[16, nb], [0, wd]], A.is_ge, 0.0, hi, -1)
+
+    def dma(q, o, i, accumulate=False):
+        eng = {"s": g.sync, "a": g.scalar, "g": g}[q]
+        if accumulate:
+            add(q, lambda: eng.dma_start(o[0], i[0], accum_op=A.add), [o], [i, o], "d")
+        else:
+            add(q, lambda: eng.dma_start(o[0], i[0]), [o], [i], "d")
+
+    def wrap(o, z, src, a, n, start=True, stop=True):
         for r in range(16):
-            mm(o, S(z, 15 - r, 143 - r), S(src, a + r, a + 16 * n, 16), r == 0, r == 15)
-
-    def split(n):
-        act(S("ya", 0, n), S("sf", 0, n), AF.Identity, bias=-7.5)
-        act(S("ya", 0, n), S("ya", 0, n), AF.Identity, bias=MAGIC)
-        act(S("ps2", 0, n), S("ya", 0, n), AF.Identity, bias=-MAGIC)
-        act(S("digb", 0, n), S("ya", 0, n), AF.Identity, bias=-MAGIC)
-
-    def unwrap(n, whole, high):
-        vtt(S("digb", 512, 512 + n), high, whole, A.subtract)
-        dma("s", S("qw", p=slice(0, 128, 16)), S("digb", 0, 256))
-        dma("s", S("qw", p=slice(15, 128, 16)), S("digb", 256, 512))
-        dma("s", S("qw", p=slice(1, 128, 16)), S("digb", 512, 768))
-        dma("a", S("qw", p=slice(14, 128, 16)), S("digb", 768, 1024))
-        mm(S("ps4", 0, 452), S("id256"), S("digb", 512, 964), True, False)
-        mm(S("ps4", 0, 452), S("id16"), S("digb", 0, 452), False, True)
+            mm(o, S(z, 15 - r, 143 - r), S(src, a + r, a + 16 * n, 16), start and r == 0, stop and r == 15)
 
     add("x", None, [S("x2", V, W)], [], "arr")
 
-    XCH = [(0, 24), (24, 56), (56, 98), (98, 146), (146, J)]
     dma("s", S("si", 0, J), H(T.up[:, :]))
     dma("a", S("si", 256, 256 + J), H(T.lo[:, :]))
     dma("s", S("x1"), H(T.x[:, :]))
-    dma("s", S("x2", 0, 384), H(T.x[:, 0:384]))
-    add("v", lambda: g.vector.memset(T["qw"][:, :], 0.0), [S("qw")], [])
+    dma("s", S("x2", 0, 16 * XCH[0][1]), H(T.x[:, 0:16 * XCH[0][1]]))
+    def clear(a, b):
+        add("v", lambda: g.vector.memset(T["qw"][:, a:b], 0.0), [S("qw", a, b)], [])
+
     iota(S("pci", 0, 1), [[0, 1]], 0, 1)
-    iota(S("si", J, 256), [[16, 256 - J]], 16 * J, 1)
-    iota(S("one"), [[0, 144]], 1, 0)
+    iota(S("gi", 0, 60), [[16, 60]], V)
+    fill(S("one"), 1)
     sel(S("idb"), S("one", 0, 128), [[-1, 128]], A.is_equal, 0.0, 0, 1)
+    rows(S("zz"), S("one"), 0, 15)
+    clear(0, 1024)
     vts(S("pci", 4, 5), S("pci", 0, 1), 15, A.bitwise_and)
-    vtt(S("col", 1, 2), S("pci", 4, 5), S("pci", 0, 1), A.subtract)
+    clear(1024, 2048)
     vcopy(S("col", 0, 1), S("pci", 4, 5))
-    vts(S("col", 5, 6), S("col", 0, 1), -1.0, A.mult)
-    vts(S("col", 6, 7), S("col", 0, 1), -1.0, A.mult, 1.0, A.add)
-    vts(S("si", 256 + J, 512), S("si", J, 256), S("col", 1, 2), A.add)
-    vcopy(S("si", J, 256), S("si", 256 + J, 512))
-    act(S("id256"), S("idb"), AF.Identity, scale=-256.0)
-    act(S("id16"), S("idb"), AF.Identity, scale=0.0625)
+    clear(2048, 3072)
+    act(S("id256"), S("idb"), scale=256.0)
+    act(S("id16"), S("idb"), scale=0.0625)
+    act(S("idn"), S("idb"), scale=-1.0)
+    for t in range(2):
+        vts(S("si", 256 * t + J, 256 * t + 256), S("gi", 0, 60), S("col", 0, 1), A.add)
+    clear(3072, W)
     vts(S("ya"), S("si"), -7.5, A.add, MAGIC, A.add)
+    vts(S("col", 1, 2), S("col", 0, 1), 1.0 / UNIT, A.mult)
     vts(S("ps2"), S("ya"), -MAGIC, A.add)
-    act(S("digb", 0, 512), S("ya"), AF.Identity, bias=-MAGIC)
-    unwrap(512, S("si"), S("ps2"))
+    act(S("digb", 0, 512), S("ya"), bias=-MAGIC)
+    vts(S("col", 2, 3), S("col", 0, 1), 8.0, A.mult)
+    vtt(S("digb", 512, 1024), S("si"), S("ps2"), A.subtract)
+    dma("a", ROW("qw", 1, 0, W), S("digb", 0, 256))
+    dma("s", ROW("qw", 2, 0, W), S("digb", 512, 768))
+    mm(S("ps4"), S("id16"), S("digb", 0, 512), True, False)
+    mm(S("ps4"), S("id256"), S("digb", 512, 1024), False, True)
     vcopy(S("q16", 0, 452), S("si", 0, 452))
-    vcopy(S("sf"), S("si"))
+    vcopy(S("pi16", 0, 452), S("ps4", 0, 452))
+    vts(S("big"), S("col", 0, 1), 13.0, A.is_ge, float(SH), A.mult)
+    vts(S("col", 3, 4), S("col", 0, 1), 256.0, A.mult)
+    dma("a", ROW("qw", 3, 0, W), S("digb", 256, 512))
+    dma("s", ROW("qw", 4, 0, W), S("digb", 768, 1024))
     for a, b in XCH[1:]:
         dma("s", S("x2", 16 * a, 16 * b), H(T.x[:, 16 * a:16 * b]))
-    iota(S("dd"), [[0, 16], [1, 16]], 0, 0)
-    iota(S("tw", 0, 16), [[16, 16]], 0, 0)
-    act(S("idn"), S("idb"), AF.Identity, scale=-1.0)
-    act(S("idm"), S("idb"), AF.Identity, scale=-8192.0)
-    act(S("nm1"), S("dd"), AF.Abs, bias=S("col", 5, 6))
-    act(S("nm2"), S("dd"), AF.Relu, bias=S("col", 6, 7))
-    act(S("tw", 0, 16), S("tw", 0, 16), AF.Identity, bias=S("col", 0, 1))
-    act(S("tw", 16, 32), S("tw", 0, 16), AF.Identity, bias=0.5)
-    act(S("tw", 32, 48), S("tw", 0, 16), AF.Identity, bias=float(R))
-    sel(S("zz"), S("one"), [[-16, 9], [0, 16]], A.is_ge, 0.0, 0, 1)
-    sel(S("m0"), S("zz", 0, 128), [[16, 8], [0, 16]], A.is_ge, 0.0, 15, -1)
-    sel(S("zz"), S("zz"), [[16, 9], [0, 16]], A.is_ge, 0.0, 15, -1)
+    sel(S("m0"), S("zz", 0, 128), [[0, 128]], A.is_ge, 0.0, 0, 0)
     sel(S("zz"), S("zz"), [[0, 9], [1, 16]], A.is_equal, 0.0, -15, 0)
-    vts(S("col", 2, 3), S("col", 0, 1), 1.0, A.is_le)
-    vts(S("col", 3, 4), S("col", 0, 1), 14.0, A.is_ge)
-    vts(S("col", 10, 11), S("col", 0, 1), -2.0, A.mult, 1.0, A.add)
-    vts(S("col", 11, 12), S("col", 0, 1), 2.0, A.mult, -29.0, A.add)
-    vtt(S("col", 2, 4), S("col", 2, 4), S("col", 10, 12), A.mult)
-    vts(S("col", 4, 5), S("col", 0, 1), 0.0, A.is_le)
-    vcopy(S("pi16", 0, 452), S("ps4", 0, 452))
-    act(S("zu"), S("zz"), AF.Identity, scale=S("col", 2, 3))
-    act(S("zl"), S("zz"), AF.Identity, scale=S("col", 3, 4))
-    act(S("z0"), S("zz"), AF.Identity, scale=S("col", 4, 5))
-    act(S("zr"), S("zz"), AF.Identity, scale=S("col", 0, 1))
+    iota(S("dd"), [[0, 16], [-8, 16]], 8)
+    iota(S("pcj"), [[1, J]], 0)
+    vts(S("pc16"), S("pcj"), S("col", 3, 4), A.add)
+    rows(S("zu1"), S("zz"), 1, 2)
+    iota(S("q2u", V, W), [[16, 60], [0, 16]], V)
+    iota(S("q2l", V, W), [[0, 60], [1, 16]], 0)
+    rows(S("zu3"), S("zz"), 3, 4)
+    for r in (2, 4):
+        dma("s", ROW("q2u", r, V, W), ROW("q2l", r, V, W))
+    for r in (1, 3):
+        dma("s", ROW("q2l", r, V, W), ROW("q2u", r, V, W))
+    for nm, src, c in (("zr", "zz", S("col", 0, 1)), ("m16", "m0", 16.0 / UNIT), ("mr", "m0", S("col", 1, 2))):
+        act(S(nm), S(src), scale=c)
+    for nm, c in (("g16", 16.0), ("g32", 32.0), ("gn16", -16.0)):
+        act(S(nm), S("m0", 0, 128, 16), scale=c)
+    act(S("nm"), S("dd"), AF.Relu, bias=S("col", 2, 3))
+    for nm, ps, c, terms in (("la", "ps0", 1.0, (("idb", 0), ("idb", 2))), ("lb1", "ps1", -16.0, (("idn", 1), ("idb", 2)))):
+        for i, (idm, k) in enumerate(terms):
+            mm(S(ps, 0, 128), S(idm), S("zz", 15 - k, 143 - k), i == 0, i == 1)
+        act(S(nm), S(ps, 0, 128), scale=c)
 
-    def late_loads():
+    def quarters(src, half):
+        act(S("eb", 0, 452), S(src, 0, 452), bias=(129.0 - half / 1024) / 4, scale=1.0 / UNIT)
+
+    def classes(rnd, ps, n, ide):
+        if rnd == 0:
+            terms = [("idq", "digb", 0), ("idq", "digb", 512), ("idq" + n, "digb", 256), ("idq" + n, "digb", 768)]
+        else:
+            terms = [("idk", "sf", 0), ("idk" + n, "sf", 256)]
+        for i, (idm, src, a) in enumerate(terms + [("idn", "eb", 0), (ide, "eb", 256)]):
+            mm(S(ps, 0, J), S(idm), S(src, a, a + J), i == 0, False)
+
+    def natural(q, a, b):
+        o, i = S("qn", 16 * a, 16 * b), IX(S("qw"), S("pc16", a, b))
+        if q == "v":
+            vcopy(o, i)
+        else:
+            act(o, i)
+
+    def lower(a, b):
+        for r in (1, 2):
+            dma("s", ROW("qn", r, W + a, W + b), ROW("qn", r + 2, a, b))
+
+    quarters("digb", 504.0)
+
+    def constants():
         dma("s", S("thi", 0, 1), H(T.th[:, :]))
         dma("s", S("sni"), H(T.snd[:, :]))
         dma("s", S("au1", V, W), H(T.x[:, V:W]))
-        iota(S("q2u", V, W), [[16, 60], [0, 16]], V, 0)
-        iota(S("q2l", V, W), [[0, 60], [-1, 16]], 0, 0)
-        iota(S("ones"), [[0, 256]], 1, 0)
+        fill(S("zero"), 0)
+        for nm, c in (("idq", 1.0 / UNIT), ("idqn", -1.0 / UNIT), ("idk", 1.0 / UNIT), ("idkn", -1.0 / UNIT)):
+            sel(S(nm), S("zero"), [[-1, 128]], A.not_equal, c, 0, 1)
         sel(S("lm"), S("m0"), [[1, 128]], A.is_gt, 0.0, 0, -1)
-        sel(S("lm"), S("lm"), [[1, 128]], A.not_equal, -512.0, 0, -1)
-        sel(S("m0f"), S("m0"), [[0, 128]], A.is_ge, 0.0, 0, 0)
-        iota(S("onef"), [[0, 128]], 1, 0)
-        for nm, c in (("m0n", -1), ("g16", 16), ("g32", 32), ("gn16", -16)):
-            n = SB[nm][0]
-            iota(S(nm), [[0, n]], c, 0)
-            sel(S(nm), S(nm), [[-16, 8], [0, n // 8]], A.is_ge, 0.0, 0, 1)
-            sel(S(nm), S(nm), [[16, 8], [0, n // 8]], A.is_ge, 0.0, 15, -1)
-        iota(S("kpat"), [[0, 16], [1, 16]], 0, 0)
-        sel(S("rs16"), S("ones"), [[0, 16], [1, 16]], A.is_gt, 0.0, 0, 0)
-        sel(S("rsbig"), S("rs16"), [[0, 16], [1, 16]], A.is_gt, 1048576.0, 0, 0)
-        sel(S("rsbig"), S("rsbig"), [[0, 16], [1, 16]], A.is_equal, 0.0, 0, 0)
-        iota(S("trow"), [[1, 256]], -512, 0)
-        iota(S("li", 0, 16), [[16, 16]], 15, 0)
-        iota(S("li", 16, 32), [[1, 16]], 0, 0)
-        iota(S("rs7"), [[0, NV * J]], 1, 0)
-        sel(S("rs7"), S("rs7"), [[0, NV], [1, J]], A.is_gt, 0.0, 0, 0)
-        iota(S("rs32"), [[0, 512]], 1, 0)
-        sel(S("rs32"), S("rs32"), [[0, 16], [1, 32]], A.is_gt, 0.0, 0, 0)
-        iota(S("c256"), [[0, J]], 256, 0)
-        for nm, a, b in (("ci", 0, JP), ("key", J, JP), ("ss", J, JP), ("hh", J, JP), ("eq", 0, 32), ("pp", 0, 264),
-                         ("ww", V, V + 16), ("rlf", R, R + CAP)):
-            iota(S(nm, a, b), [[0, b - a]], 0, 0)
-        iota(S("iov"), [[1, V + 16]], 0, 0)
-
-    def later_loads():
-        dma("s", S("q2u", V, W, p=slice(1, 128, 16)), S("q2l", V, W, p=slice(1, 128, 16)))
-        dma("s", S("q2l", V, W, p=slice(15, 128, 16)), S("q2u", V, W, p=slice(15, 128, 16)))
-        dma("s", S("al", V, W), H(T.x[:, V:W]))
-
-    PCH = [(0, 66), (66, 132), (132, J)]
-    UCH = [(0, 64), (64, 128), (128, J)]
-    LCH = [(0, 64), (64, 128), (128, 176), (176, J)]
-    bank = [0]
+        sel(S("lm"), S("lm"), [[1, 128]], A.not_equal, -256.0, 0, -1)
+        iota(S("trow"), [[1, 256]], 0)
+        iota(S("trm"), [[1, 256]], -256)
+        for nm, a, b, c in (("bad", J, JP, 0), ("sc", 0, 8, 0), ("ul", J, JW, 0), ("key", J, JW, 0), ("hh", J, JW, 0),
+                            ("bw", 0, JW, SH), ("ww", V, V + 16, 0), ("rlf", R, R + CAP, 0), ("n64", 0, 256, -65)):
+            fill(S(nm, a, b), c)
+        iota(S("kpat"), [[0, 16], [1, 16]], 0)
+        fill(S("rsbig"), 0)
+        sel(S("rsbig"), S("rsbig"), [[0, 16], [1, 16]], A.not_equal, 1048576.0, 0, 0)
+        iota(S("li"), [[1, 16]], 0)
+        iota(S("dump", 0, 16), [[16, 16]], R - SH)
+        iota(S("dump", 16, 32), [[16, 16]], 2 * W - SH)
+        iota(S("dump", 32, 48), [[16, 16]], R - SH)
+        iota(S("dump", 48, 64), [[16, 16]], 2 * V - SH)
+        fill(S("qn", W, 2 * W + CAP), 0)
 
     def level(o, src, own, lst, base, a, b, copy=None):
         vtt(S(o, 16 * a, 16 * b), IX(S(src), S(lst, base + a, base + b)), S(own, 16 * a, 16 * b), A.max)
         if copy:
             dma("s", S(copy, 16 * a, 16 * b), S(o, 16 * a, 16 * b))
 
-    def levels(o, src, own, lst, base, copy):
-        for a, b in ((0, 98), (98, J)):
-            level(o, src, own, lst, base, a, b, copy)
-
-    def chase(o, src, lst, base, z, ps, between=None):
-        for a, b in PCH:
-            act(S(o, 16 * a, 16 * b), IX(S(src), S(lst, base + a, base + b)), AF.Identity)
-            if between and b == J:
-                between()
+    def chase(o, win, lst, base, z, ps, parts, meanwhile=None):
+        for a, b in parts:
+            act(S(o, 16 * a, 16 * b), IX(win, S(lst, base + a, base + b)))
+            if meanwhile:
+                meanwhile()
             wrap(S(ps, a, b), z, o, 16 * a, b - a)
 
-    def distance(m, ab, a, b):
-        n = (b - a + 31) // 32
-        cut = [a + (b - a) * i // n for i in range(n + 1)]
-        for i in range(n):
-            c0, c1 = 16 * cut[i], 16 * cut[i + 1]
-            pb = S("ps%d" % (bank[0] % 3), 0, c1 - c0)
-            bank[0] += 1
-            mm(pb, S("idn"), S("ww", c0, c1), True, False)
-            mm(pb, S("idb"), S(m, c0, c1), False, True)
-            act(S(ab, c0, c1), pb, AF.Abs)
+    def minus(i, m, a, b):
+        for idm, src in (("idn", "ww"), ("idb", m)):
+            for c in range(16 * a, 16 * b, 512):
+                e = min(c + 512, 16 * b)
+                mm(S("ps%d" % (2 * i + (c - 16 * a) // 512), 0, e - c), S(idm), S(src, c, e), src == "ww", src != "ww")
+
+    def size(i, ab, a, b):
+        act(S(ab, 16 * a, 16 * b), P2(i, 16 * (b - a)), AF.Abs)
 
     def merge(au, a, b):
         for k in range(8):
-            rows = slice(16 * k + 8, 16 * k + 16)
-            dma("s", S(au, a, b, p=rows), S("al", a, b, p=rows))
+            rw = slice(16 * k + 8, 16 * k + 16)
+            dma("s", S(au, a, b, p=rw), S("al", a, b, p=rw))
 
-    def rhyme_write():
-        for q in range(7, -1, -1):
+    def rhyme_write(batches, between):
+        for q in batches:
             vtt(IX(S("rlf"), S("of16", 2 * q, 2 * q + 2)), S("zd", 32 * q, 32 * q + 32), S("caf", 32 * q, 32 * q + 32), A.add)
+            if between:
+                between.pop(0)()
 
-    def pointers(o):
-        vtt(S("ze"), S("ps1", 0, 256), S("ee"), A.mult)
-        vscan(S("pp", 1, 257), S("ones"), S("ze"), A.mult, A.add)
-        vcopy(S("gg"), IX(S("pp"), S("cj16", 0, 13)))
-        vtt(S("ps2", 0, J), S("gg", 1, J + 1), S("gg", 0, J), A.subtract)
-        vtt(S("ps3", 0, J), S("ps2", 0, J), S("ul", 0, J), A.mult)
-        vtt(S("ps3", 256, 452), S("ps2", 0, J), S("ul", J, 2 * J), A.mult)
-        vtt(S(o, 0, J), S("ps3", 0, J), S("sf", 0, J), A.add)
-        vtt(S(o, 256, 452), S("ps3", 256, 452), S("sf", 256, 452), A.add)
+    far = [d for d in range(1, N) if topo.chip(T.cores[(rank + d) % N]) != topo.chip(core)]
+    out = topo.engines(core, T.cores[(rank + far[0]) % N])
+    per = len(out) // len(far)
+    eng = {d: out[per * i:per * i + per] for i, d in enumerate(far)}
+    for d in range(1, N):
+        if d not in far:
+            eng[d] = [e for e in topo.engines(core, T.cores[(rank + d) % N]) if e not in out]
+    total = sum(len(eng[d]) for d in eng)
+
+    def send():
+        act(S("sbuf"), IX(S("au1"), S("sn16")))
+        trs = []
+        for d in range(1, N):
+            rid, pid, _ = topo.addr(T.cores[(rank + d) % N])
+            trs.append(RemoteDMATransfer(dst_ids=[DstId(rid=rid, pnc=pid)], dma_engine_mask=sum(1 << e for e in eng[d]),
+                                         remote_sem=T.sem.arr, src=T["sbuf"][:, (d - 1) * G:d * G],
+                                         dst=T["x2"][:, V + (d - 1) * G:V + d * G]))
+        add("g", lambda: g.remote_dma_fused(trs, local_sem=T.sem.sent), [], [S("sbuf")], "r")
 
     for rnd in range(2):
         xs, xo, au = ("x1", "x2", "au1") if rnd == 0 else ("x2", "x1", "au2")
+        wu, wl, zl, pl = (S("qw"), S("qw"), "zu3", "pi16") if rnd == 0 else (S("qn", 0, W), S("qn", W, 2 * W), "zu1", "q16")
         thr = S("col", 8 + rnd, 9 + rnd)
         if rnd == 0:
-            late_loads()
+            constants()
             for a, b in XCH[:3]:
                 level(au, xs, xo, "q16", 0, a, b)
-        else:
-            split(452)
-            vcopy(S("q16", 0, 452), S("sf", 0, 452))
-            level(au, xs, xo, "q16", 0, 0, 40)
-            unwrap(452, S("sf", 0, 452), S("ps2", 0, 452))
-            level(au, xs, xo, "q16", 0, 40, 60)
-            vcopy(S("pi16", 0, 452), S("ps4", 0, 452))
-            level(au, xs, xo, "q16", 0, 60, 98)
-        dma("s", S("cu", 0, 1568), S(au, 0, 1568))
-        level(au, xs, xo, "q16", 0, 98, 146)
-        level(au, xs, xo, "q16", 0, 146, J)
-        dma("s", S("cu", 1568, V), S(au, 1568, V))
-        if rnd == 0:
-            later_loads()
-        chase("q2u", "qw", "pi16", 0, "zu", "ps3")
-        levels("al", xs, xo, "q16", 256, "cl")
-        vcopy(S("p2u"), S("ps3", 0, J))
-        chase("q2l", "qw", "pi16", 256, "zl", "ps4")
-        if rnd == 0:
+            dma("s", S("cu", 0, 1568), S(au, 0, 1568))
+            for a, b in XCH[3:]:
+                level(au, xs, xo, "q16", 0, a, b)
+            dma("s", S("cu", 1568, V), S(au, 1568, V))
             dma("s", S("bu", V, W), H(T.x[:, V:W]))
-            dma("s", S("ww", 0, V), H(T.w[:, :]))
-        levels("bu", au, "cu", "p2u", 0, "cu")
+            dma("s", S("ww", 0, 1568), H(T.w[:, 0:1568]))
+        else:
+            for (a, b, o), (c, e) in zip(((0, 64, 0), (64, J, 1024), (256, 256 + J, W)), ((0, 48), (48, 130), (130, J))):
+                wrap(S("ps6", a, b), "zu1", "qn", o, b - a)
+                vcopy(S("q16", a, b), S("ps6", a, b))
+                level(au, xs, xo, "q16", 0, c, e, "cu")
+        chase("q2u", wu, pl, 0, "zu1", "ps4", HALF if rnd == 0 else FIRST)
+        chase("q2l", wl, pl, 256, zl, "ps5", [(0, 50)])
+        level("al", xs, xo, "q16", 256, 0, 50)
+        vcopy(S("p2u"), S("ps4", 0, J))
+        chase("q4", S("q2u"), "p2u", 0, "zu1", "ps7", HALF)
+        level("al", xs, xo, "q16", 256, 50, 122)
+        level("al", xs, xo, "q16", 256, 122, J)
+        dma("s", S("cl", 0, 2048), S("al", 0, 2048))
+        chase("q2l", wl, pl, 256, zl, "ps5", [(50, 122), (122, J)])
+        for a, b in THIRD:
+            if b == J:
+                vcopy(S("p4u"), S("ps7", 0, J))
+            level("bu", au, "cu", "p2u", 0, a, b, "cu")
+        if rnd == 0:
+            dma("s", S("al", V, W), H(T.x[:, V:W]))
+            dma("s", S("ww", 1568, V), H(T.w[:, 1568:V]))
+        dma("s", S("cl", 2048, V), S("al", 2048, V))
         if rnd == 0:
             dma("s", S("bl", V, W), H(T.x[:, V:W]))
-        vcopy(S("p2l"), S("ps4", 0, J))
-        chase("q4", "q2u", "p2u", 0, "zu", "ps3")
-        levels("bl", "al", "cl", "p2l", 0, "cl")
-        vcopy(S("p4u"), S("ps3", 0, J))
+            natural("a", *NAT[0])
+        else:
+            act(S("sf", 0, 452), S("ps6", 0, 452))
+            quarters("sf", 511.5)
+            for t in range(2):
+                dma("s", ROW("pt", 0, V * t, V * t + V), S("sf", 256 * t, 256 * t + J))
+        level(au, "bu", "cu", "p4u", 0, 0, 32)
+        vcopy(S("p2l"), S("ps5", 0, J))
+        level(au, "bu", "cu", "p4u", 0, 32, 98)
+        level(au, "bu", "cu", "p4u", 0, 98, J)
+        classes(rnd, "ps4", "n", "idb")
+        classes(rnd, "ps7", "", "idn")
+        def first():
+            minus(0, au, 0, 49)
+            minus(1, au, 49, 98)
+
+        def second():
+            minus(0, au, 98, 147)
+            minus(1, au, 147, J)
+            wrap(S("ps5", 0, 98), "zz", "abu", 0, 98)
+
+        chase("q4", S("q2l"), "p2l", 0, zl, "ps6", HALF[:1], first)
+        size(0, "abu", 0, 49)
+        size(1, "abu", 49, 98)
+        chase("q4", S("q2l"), "p2l", 0, zl, "ps6", HALF[1:], second)
+        size(0, "abu", 98, 147)
+        size(1, "abu", 147, J)
         if rnd == 0:
             dma("s", S("rli"), H(T.rl[:, :]))
-            vcopy(thr, S("thi", 0, 1))
-        for a, b in UCH:
-            level(au, "bu", "cu", "p4u", 0, a, b)
-        chase("q4", "q2l", "p2l", 0, "zl", "ps4", lambda au=au: distance(au, "abu", 0, 64))
-        vcopy(S("p4l"), S("ps4", 0, J))
-        distance(au, "abu", 64, 128)
-        wrap(S("ps5", 0, 64), "zz", "abu", 0, 64)
-        distance(au, "abu", 128, J)
-        wrap(S("ps5", 64, 128), "zz", "abu", 1024, 64)
+        for a, b in THIRD:
+            level("bl", "al", "cl", "p2l", 0, a, b, "cl")
+        vcopy(S("p4l"), S("ps6", 0, J))
+        if rnd == 0:
+            sel(S("rlf", 0, R), S("rli"), [[0, R]], A.is_ge, 0.0, 0, 0)
+
+        def piece(i):
+            return S("ps%d" % (i % 4), 0, 16 * (LCH[i][1] - LCH[i][0]))
+
+        def witness(i):
+            if i < len(LCH):
+                mm(piece(i), S("idn"), S("ww", 16 * LCH[i][0], 16 * LCH[i][1]), True, False)
+
+        for i in range(3):
+            witness(i)
+        wrap(S("ps5", 98, J), "zz", "abu", 1568, 98)
         for i, (a, b) in enumerate(LCH):
             level("al", "bl", "cl", "p4l", 0, a, b)
-            distance("al", "abl", a, b)
-            if i == 0:
-                wrap(S("ps5", 128, J), "zz", "abu", 2048, J - 128)
-            if i == 1:
-                act(S("thru"), S("ps5", 0, J), AF.Identity, bias=thr, scale=-1.0)
-                act(S("dus"), S("ps5", 0, J), AF.Identity)
-                merge(au, 0, 2048)
-                wrap(S("ps6", 0, 64), "zz", "abl", 0, 64)
-        wrap(S("ps6", 64, 128), "zz", "abl", 1024, 64)
-        wrap(S("ps6", 128, J), "zz", "abl", 2048, J - 128)
-        merge(au, 2048, V)
-        mm(S("ps1", 0, 256), S("idm"), S("nm1"), True, False)
-        vtt(S("ps7", 0, J), S("sf", 0, J), S("sf", 256, 256 + J), A.subtract)
+            mm(piece(i), S("idb"), S("al", 16 * a, 16 * b), False, True)
+            act(S("abl", 16 * a, 16 * b), piece(i), AF.Abs)
+            witness(i + 3)
+            for after, c, e in LSUM:
+                if after == i:
+                    wrap(S("ps6", c, e), "zz", "abl", 16 * c, e - c)
+            for after, c, e in LMERGE:
+                if after == i:
+                    merge(au, 16 * c, 16 * e)
+        def upper_sums():
+            return [lambda: vts(S("thru"), S("ps5", 0, J), -1.0, A.mult, thr, A.add), lambda: vcopy(S("dus"), S("ps5", 0, J))]
+
         if rnd == 0:
-            vcopy(S("rlf", 0, R), S("rli"))
+            vcopy(thr, S("thi", 0, 1))
             vcopy(S("sn16"), S("sni"))
-            vcopy(S("l16"), S("li"))
+            for f in upper_sums():
+                f()
+            natural("v", *NAT[1])
+            natural("a", *NAT[2])
         else:
-            rhyme_write()
-            dma("s", H(T.y[:, :]), S(au, 0, V))
-        vtt(S("bad"), S("ps6", 0, J), S("thru"), A.is_gt)
-        mm(S("ps3", 0, J), S("m0"), S("bad"))
-        mm(S("ps4", 0, J), S("lm"), S("bad"))
+            rhyme_write(range(6, 3, -1), upper_sums())
+        vtt(S("bad", 0, J), S("ps6", 0, J), S("thru"), A.is_gt)
+        vscan(S("sc", 8, 8 + JP), S("bad"), S("bad"), A.add, A.max)
         vtt(S("ul", 0, J), S("ps6", 0, J), S("dus"), A.is_le)
-        vscan(S("ci", 1, J + 1), S("ps3", 0, J), S("c256"), A.add, A.min)
-        for a in range(NV, 16):
-            act(S("junk", a * J, a * J + J), S("ci", 1, J + 1), AF.Sign, bias=S("tw", 16 + a, 17 + a), scale=-1.0,
-                acc=S("acc", a, a + 1))
-        vtt(S("ps7", 256, 256 + J), S("ps7", 0, J), S("ul", 0, J), A.mult)
-        for a in range(NV):
-            vts(S("cmp", a * J, a * J + J), S("ci", 1, J + 1), S("tw", a, a + 1), A.is_le)
-        wrap(S("ps5", 0, 13), "z0", "ci", 0, 13)
-        vtt(S("ss", 0, J), S("ps7", 256, 256 + J), S("sf", 256, 256 + J), A.add)
-        vscan(S("cms"), S("rs7"), S("cmp"), A.mult, A.add)
-        vtt(S("key", 0, J), S("ps4", 0, J), S("ci", 0, J), A.add)
-        vcopy(S("jf", 0, NV), S("cms", J - 1, NV * J, J))
-        act(S("jf", NV, 16), S("acc", NV, 16), AF.Identity, bias=J / 2.0, scale=0.5)
-        vts(S("hh", 0, J), S("ss", 0, J), R - 1, A.bitwise_and)
-        vcopy(S("j16"), S("jf", 0, 16))
-        act(S("jf", 16, 32), S("jf", 0, 16), AF.Identity, scale=16.0)
-        if rnd == 0:
-            act(S("sbuf"), IX(S(au), S("sn16")), AF.Identity)
-            far = [d for d in range(1, N) if topo.chip(T.cores[(rank + d) % N]) != topo.chip(core)]
-            out = topo.engines(core, T.cores[(rank + far[0]) % N])
-            per = len(out) // len(far)
-            eng = {d: out[per * i:per * i + per] for i, d in enumerate(far)}
-            for d in range(1, N):
-                if d not in far:
-                    eng[d] = [e for e in topo.engines(core, T.cores[(rank + d) % N]) if e not in out]
-            total = sum(len(eng[d]) for d in eng)
-            trs = []
-            for d in range(1, N):
-                rid, pid, _ = topo.addr(T.cores[(rank + d) % N])
-                trs.append(RemoteDMATransfer(dst_ids=[DstId(rid=rid, pnc=pid)], dma_engine_mask=sum(1 << e for e in eng[d]),
-                                             remote_sem=T.sem.arr, src=T["sbuf"][:, (d - 1) * G:d * G],
-                                             dst=T["x2"][:, V + (d - 1) * G:V + d * G]))
-            add("g", lambda trs=trs: g.remote_dma_fused(trs, local_sem=T.sem.sent), [], [S("sbuf")], "r")
-            for b in ("au2", "al", "bu", "bl"):
-                dma("s", S(b, V, W), S("x2", V, W))
-        vtt(S("ee"), IX(S("key"), S("j16")), S("trow"), A.is_equal)
+        if rnd == 1:
+            dma("s", H(T.y[:, :]), S(au, 0, V))
+        else:
+            send()
+            dma("s", S("qn", V, W), S("q2u", V, W))
+            lower(0, 16 * NAT[2][1])
+            lower(V, W)
+        mm(S("ps0", 0, 1), S("idb"), S("big"), True, False)
+        for a in range(13):
+            mm(S("ps0", 0, 1), S("zz", 15 - a, 143 - a), S("sc", 16 * a + 23, 16 * a + 24), False, a == 12)
+        wrap(S("ps1", 0, 13), "zz", "sc", 8, 13)
+        vts(S("cm1"), S("trow"), S("ps0", 0, 1), A.is_ge, 16.0, A.mult)
+        if rnd == 1:
+            rhyme_write([3, 2], [])
+        else:
+            vts(S("dump"), S("dump"), S("col", 0, 1), A.add, 1.0 / SH, A.mult)
+            vcopy(S("l16"), S("li"))
+        act(S("bw", 0, JP, 16), S("ps1", 0, 13))
+        wrap(S("ps3", 0, 16), "zz", "cm1", 0, 16)
+        mm(S("ps2", 0, J), S("m0"), S("sc", 7, 7 + J), True, False)
+        mm(S("ps2", 0, J), S("lm"), S("bad", 0, J), False, True)
+        mm(S("ps4", 0, J), S("idb"), S("ul", 0, J), False, True)
+        wrap(S("ps5", 0, 16), "zz", "cm1", 0, 16, True, False)
+        vcopy(S("a16"), S("ps3", 0, 16))
+        vtt(S("cm2"), IX(S("bw"), S("a16")), S("trow"), A.is_le)
+        if rnd == 1:
+            rhyme_write([1, 0], [])
+        act(S("key", 0, J), S("ps2", 0, J))
+        act(S("ra"), S("ps4", 0, J), AF.Abs, bias=-UNIT / 2, scale=UNIT)
+        wrap(S("ps5", 0, 16), "zz", "cm2", 0, 16, False, True)
+        mm(S("ps7", 0, J), S("idk"), S("ra"), False, True)
+        vcopy(S("j16"), S("ps5", 0, 16))
+        act(S("tiny", 0, 16), S("ps5", 0, 16), scale=16.0 * UNIT)
+        act(S("hh", 0, J), S("ps7", 0, J), bias=258.0 * 512 - 1023.0, scale=UNIT / 2)
+        if rnd == 1:
+            act(S("tiny", 16, 32), S("ps5", 0, 16), scale=-3135.0 * UNIT / SH)
+        vtt(S("ee"), IX(S("key"), S("j16")), S("trm"), A.is_equal)
         vtt(S("zh"), IX(S("hh"), S("j16")), S("ee"), A.mult)
-        wrap(S("ps0", 0, 16), "zr", "ee", 0, 16)
-        mm(S("ps1", 0, 256), S("m0f"), S("zh"), False, True)
-        vtt(S("jf", 32, 48), S("ps0", 0, 16), S("jf", 16, 32), A.add)
-        vcopy(S("v16"), S("jf", 32, 48))
-        act(S("wv"), IX(S("ww"), S("v16")), AF.Identity)
-        vscan(S("hsc"), S("rs16"), S("ps1", 0, 256), A.mult, A.max)
-        vcopy(S("h16"), S("hsc", 15, 256, 16))
-        act(S("hw"), S("hsc", 15, 256, 16), AF.Identity)
+        act(S("tj"), IX(S("ul"), S("j16")))
+        mm(S("ps1", 0, 16), S("idk"), S("tiny", 0, 16), True, False)
+        wrap(S("ps1", 0, 16), "zr", "ee", 0, 16, False, True)
+        wrap(S("ps0", 0, 16), "zz", "zh", 0, 16)
+        vts(S("v16"), S("ps1", 0, 16), float(V), A.min)
+        act(S("wv"), IX(S("ww"), S("v16")))
+        act(S("tiny", 32, 48), S("ps1", 0, 16), scale=(1.0, 196.0)[rnd] * UNIT / SH)
+        vts(S("h16"), S("ps0", 0, 16), -1.0, A.add)
+        vcopy(S("ca16"), IX(S("rlf"), S("h16")))
+        act(S("tiny", 48, 64), S("ps0", 0, 16), bias=-UNIT / SH, scale=UNIT / SH)
+        act(S("val"), S("ps0", 0, 16), AF.Sign)
+        act(S("xh"), IX(S("tiny", 48, 64), S("l16")), bias=1.0, scale=SH / UNIT)
+        act(S("caf"), IX(S("rlf"), S("h16")))
+        mm(S("ps7", 0, 256), S("id256"), S("nm"), True, False)
+        mm(S("ps7", 0, 256), S("m0"), S("zh"), False, True)
+        mm(S("ps7", 256, 496), S("m0"), S("zh", 16, 256))
         mm(S("ps6", 0, 128), S("idb"), S("wv", 0, 128))
         mm(S("ps4", 0, 256), S("idb"), S("kpat"), True, False)
-        vcopy(S("ca16"), IX(S("rlf"), S("h16")))
-        act(S("xh"), IX(S("hw"), S("l16", 16, 32)), AF.Identity)
-        mm(S("ps7", 0, 256), S("m0f"), S("zh"))
-        mm(S("ps7", 256, 512), S("idm"), S("nm2"), True, False)
-        mm(S("ps7", 256, 512), S("m0f"), S("zh"), False, True)
-        vcopy(S("yc", 0, 16 * TV), IX(S(au), S("ca16", 0, TV)))
-        for c in range(2):
-            t0 = TV if c == 0 else 192
-            act(S("yc", 16 * t0, 3072 + 1024 * c), IX(S(au), S("ca16", t0, 192 + 64 * c)), AF.Identity)
+        mm(S("ps5", 0, 256), S("idb"), S("ee"), True, False)
+        mm(S("ps5", 0, 256), S("idn"), S("tj"), False, True)
+        mm(S("ps6", 256, 512), S("m16"), S("cm1"), True, False)
+        mm(S("ps6", 256, 512), S("m16"), S("cm2"), False, False)
+        mm(S("ps6", 256, 512), S("mr"), S("ee"), False, False)
+        mm(S("ps6", 256, 512), S("idkn"), S("caf"), False, True)
+        vcopy(S("yc", 0, 16 * TE), IX(S(au), S("ca16", 0, TE)))
+        vtt(S("eq", 0, 256), S("ps7", 0, 256), S("xh"), A.is_equal)
+        vtt(S("eq", 256, 496), S("ps7", 256, 496), S("xh", 0, 240), A.is_equal)
+
+        def places(ps, a):
+            vtt(S("tiny", 64 + a, 80 + a), S(ps, 0, 16), S("dump", 32 * rnd + a, 32 * rnd + a + 16), A.min)
+            return lambda: vts(S("of16", a, a + 16), S("tiny", 64 + a, 80 + a), 1.0, A.add, float(SH), A.mult)
+
+        def differ(c, witness):
             for k in range(16):
-                o = S("ps%d" % (k // 4), 128 * (k % 4) + 64 * c, 128 * (k % 4) + 64 * c + 64)
-                mm(o, S("idn"), S("wv", 128 + 64 * c, 192 + 64 * c), True, False)
-                mm(o, S("idb"), S("yc", 2048 + 1024 * c + k, 3072 + 1024 * c, 16), False, True)
-            if c == 0:
-                for k in range(16):
-                    mm(S("ps4", k, 128, 16), S("yc", k, 2048, 16), S("gn16"), False, False)
-        vcopy(S("cj16", 0, 13), S("ps5", 0, 13))
-        vtt(S("eq", 0, 512, 2), S("ps7", 256, 512), S("xh"), A.is_equal)
-        vtt(S("eq", 33, 512, 2), S("ps7", 0, 240), S("xh", 16, 256), A.is_equal)
-        vtt(S("zs"), IX(S("ss"), S("j16")), S("ee"), A.mult)
-        vscan(S("eqs"), S("rs32"), S("eq"), A.mult, A.add)
-        vts(S("tiny", 0, 16), S("tw", 0, 16), S("ci", J, J + 1), A.is_lt)
-        for b in range(4):
-            act(S("abd", 512 * b, 512 * b + 512), S("ps%d" % b), AF.Abs)
-            for k in range(4 * b, 4 * b + 4):
-                vtt(S("mx", 128 * k, 128 * k + 128), S("ps6", 0, 128), S("yc", k, 2048, 16), A.max)
-            if b == 0:
-                vtt(S("tiny", 16, 32), S("eqs", 31, 512, 32), S("tiny", 0, 16), A.is_ge)
-            if b == 1:
-                vtt(S("tiny", 32, 48), S("tiny", 16, 32), S("tw", 32, 48), A.mult)
-            if b == 2:
-                vtt(S("tiny", 48, 64), S("tiny", 32, 48), S("hw"), A.max)
-            if b == 3:
-                vcopy(S("of16"), S("tiny", 48, 64))
-            for k in range(4 * b, 4 * b + 4):
-                mm(S("ps4", k, 128, 16), S("mx", 128 * k, 128 * k + 128), S("g32"), False, False)
-            for k in range(4 * b, 4 * b + 4):
-                mm(S("ps4", 128 + k, 256, 16), S("abd", 128 * k, 128 * k + 128), S("g16"), False, k == 15)
-        act(S("caf"), IX(S("rlf"), S("h16")), AF.Identity)
-        act(S("ul", J, 2 * J), S("ul", 0, J), AF.Identity, bias=1.0, scale=-1.0)
-        vscan(S("pm"), S("rsbig"), S("ps4", 0, 256), A.add, A.min)
-        mm(S("ps1", 0, 256), S("m0n"), S("zs"), True, False)
+                ps = "ps%d" % (2 * c + k // 8)
+                o = S(ps, 64 * (k % 8), 64 * (k % 8) + 64)
+                if witness and k % 8 == 0:
+                    mm(S(ps), S("zero"), S("ww", 0, 512), True, False)
+                if witness:
+                    mm(o, S("idn"), S("wv", 128 + 64 * c, 192 + 64 * c), False, False)
+                else:
+                    mm(o, S("idb"), S("yc", 2048 + 1024 * c + k, 3072 + 1024 * c, 16), False, k % 8 == 7)
+
+        def keys(c, ks, stop=False):
+            for k in ks:
+                if c < 2:
+                    mm(S("ps4", 128 + k, 256, 16, p=slice(64 * c, 64 * c + 64)),
+                       S("abd", 1024 * c + 64 * k, 1024 * c + 64 * k + 64), S("g16"), False, stop and k == ks[-1])
+                else:
+                    mm(S("ps4", k, 128, 16), S("mx", 128 * k, 128 * k + 128), S("g32"), False, stop and k == ks[-1])
+
+        vcopy(S("yc", 16 * TE, 2048), IX(S(au), S("ca16", TE, 128)))
+        act(S("yc", 2048, 3072), IX(S(au), S("ca16", 128, 192)))
+        act(S("yc", 3072, W), IX(S(au), S("ca16", 192, 256)))
+        differ(0, True)
+        differ(1, True)
+        differ(0, False)
+        for k in range(16):
+            mm(S("ps4", k, 128, 16), S("yc", k, 2048, 16), S("gn16"), False, False)
+        differ(1, False)
+        act(S("abd", 0, 1024), P2(0, 1024), AF.Abs)
+        act(S("abd", 1024, 1536), S("ps2"), AF.Abs)
+        act(S("abd", 1536, 2048), S("ps3"), AF.Abs)
+        act(S("te"), S("ps5", 0, 256), AF.Relu, scale=float((W, V)[rnd]) / SH)
+        for k in range(16):
+            vtt(S("mx", 128 * k, 128 * k + 128), S("ps6", 0, 128), S("yc", k, 2048, 16), A.max)
+        keys(0, range(16))
+        keys(2, range(8))
+        keys(1, range(8))
+        keys(2, range(8, 15))
+        keys(1, range(8, 16))
+        keys(2, [15], True)
+        act(S("dv"), S("ps6", 256, 512), scale=UNIT)
+
+        def rhyme_places():
+            mm(S("ps7", 0, 16), S("idk"), S("tiny", 48, 64), True, False)
+            mm(S("ps7", 0, 16), S("idn"), S("val"), False, False)
+            wrap(S("ps7", 0, 16), "zz", "eq", 0, 16, False, False)
+            wrap(S("ps7", 1, 16), "zz", "eq", 256, 15, False, True)
+
+        def table_places():
+            mm(S("ps5", 0, 16), S("idn"), S("val"), True, False)
+            wrap(S("ps5", 0, 16), "zz", "te", 0, 16, False, False)
+            if rnd == 1:
+                mm(S("ps5", 0, 16), S("idk"), S("tiny", 16, 32), False, False)
+            mm(S("ps5", 0, 16), S("idk"), S("tiny", 32, 48), False, True)
+
         if rnd == 0:
-            act(S("junk", 0, J), S("bad"), AF.Identity, acc=S("cnt", 0, 1))
-        vcopy(S("pmx"), IX(S("pm"), S("l16", 0, 16)))
-        vtt(S("oh"), S("ps4", 0, 256), S("pmx"), A.is_equal)
+            natural("a", *NAT[3])
+            lower(16 * NAT[3][0], V)
+            vts(S("cah"), S("caf"), 0.0625, A.mult, 1039.53125, A.add)
+            mm(S("ps0", 0, 256), S("lb1"), S("n64"), True, False)
+            table_places()
+        else:
+            rhyme_places()
+        vscan(S("ps1", 0, 256), S("rsbig"), S("ps4", 0, 256), A.add, A.min)
+        vscan(REV("pmx"), S("rsbig"), (T["ps4"][:, 255::-1], S("ps4", 0, 256)[1]), A.add, A.min)
+        vtt(S("oh"), S("ps1", 0, 256), S("pmx"), A.is_equal)
         for h in range(2):
             mm(S("ps6", 128 * h, 128 * h + 128), S("oh", 128 * h, 128 * h + 128), S("idb"))
-        vtt(S("dv"), IX(S("iov"), S("v16")), S("caf"), A.subtract)
-        vtt(S("zc"), S("ps6", 0, 256), S("caf"), A.mult)
-        mm(S("ps1", 0, 256), S("m0f"), S("zc"), False, True)
-        vtt(S("zd"), S("ps6", 0, 256), S("dv"), A.mult)
+        then = places("ps5", 16) if rnd == 0 else places("ps7", 0)
+        then()
         if rnd == 0:
-            mm(S("ps5", 100, 101), S("onef"), S("cnt", 0, 1))
-            act(S("cnt", 1, 2), S("ps5", 100, 101), AF.Identity, bias=-7.5)
-            act(S("cnt", 2, 3), S("cnt", 1, 2), AF.Identity, bias=MAGIC)
-            act(S("cnt", 3, 4), S("cnt", 2, 3), AF.Identity, bias=MAGIC, scale=-1.0)
-            act(S("cnt", 4, 5), S("ps5", 100, 101), AF.Identity, bias=S("cnt", 3, 4))
-            act(S("col", 9, 10), S("cnt", 4, 5), AF.Identity, bias=S("col", 8, 9))
-            pointers("sf")
+            vtt(S("zc"), S("ps6", 0, 256), S("caf"), A.mult)
+            vtt(S("zch"), S("ps6", 0, 256), S("cah"), A.mult)
+            mm(S("ps0", 0, 256), S("la"), S("zc"), False, False)
+            mm(S("ps0", 0, 256), S("lb1"), S("zch"), False, True)
+            rhyme_places()
+            vtt(S("zd"), S("ps6", 0, 256), S("dv"), A.mult)
+            act(S("crb"), S("ps0", 0, 256))
+            vcopy(IX(S("qn"), S("of16", 16, 32)), S("crb"))
+            places("ps7", 0)()
+            rhyme_write([7], [])
+            for b in ("au2", "al", "bu", "bl"):
+                dma("s", S(b, V, W), S("x2", V, W))
+            mm(S("ps1", 0, 1), S("one", 0, 128), S("sc", 7 + JP, 8 + JP))
+            act(S("cnt", 1, 2), S("ps1", 0, 1), bias=-7.5)
+            act(S("cnt", 2, 3), S("cnt", 1, 2), bias=MAGIC)
+            act(S("cnt", 3, 4), S("cnt", 2, 3), bias=MAGIC, scale=-1.0)
+            act(S("cnt", 4, 5), S("ps1", 0, 1), bias=S("cnt", 3, 4))
+            act(S("col", 9, 10), S("cnt", 4, 5), bias=S("col", 8, 9))
         else:
-            rhyme_write()
+            def chosen():
+                vtt(S("zc"), S("ps6", 0, 256), S("caf"), A.mult)
+                mm(S("ps0", 0, 256), S("la"), S("zc"))
+                act(S("crow"), S("ps0", 0, 256))
+
+            def table(a, b):
+                return lambda: vcopy(IX(S("pt"), S("of16", 16 + a, 16 + b)), S("crow", 16 * a, 16 * b))
+
+            def pointers():
+                table(12, 16)()
+                dma("s", H(T.up1[:, :]), ROW("pt", 0, 0, V))
+                dma("a", H(T.lo1[:, :]), ROW("pt", 0, V, 2 * V))
+
+            table_places()
+            chosen()
+            vtt(S("zd"), S("ps6", 0, 256), S("dv"), A.mult)
+            later = [places("ps5", 16)]
+            rhyme_write(range(7, -1, -1), later + [lambda: None, table(0, 4), table(4, 8), table(8, 12), pointers])
             dma("s", H(T.rl1[:, 0:512]), S("rlf", 0, 512))
             dma("a", H(T.rl1[:, 512:R]), S("rlf", 512, R))
-            pointers("po")
-            dma("s", H(T.up1[:, :]), S("po", 0, J))
-            dma("a", H(T.lo1[:, :]), S("po", 256, 452))
 
     emit(g, T, ops, total)
 
@@ -476,26 +618,25 @@ def emit(g, T, ops, total):
     for i, (q, fn, rd, wr, kind) in enumerate(ops):
         need = {}
         for regions, w in ((rd, False), (wr, True)):
-            for name, a, b in regions:
-                psum = name.startswith("ps")
-                for j, w2, a2, b2 in seen.get(name, []):
+            for name, a, b, m in regions:
+                psum = name in PSUM
+                for j, w2, a2, b2, m2 in seen.get(name, []):
+                    if need.get(src[j], -1) >= j:
+                        continue
                     same = ops[j][4] == "c" and kind == "c" and ops[j][0] == q
                     if psum and not same:
                         hit = True
-                    elif same and q == "t":
+                    elif (same and q == "t") or not m & m2:
                         hit = False
                     elif w and w2 and (kind == "c") != (ops[j][4] == "c"):
                         hit = a // 16 < -(-b2 // 16) and a2 // 16 < -(-b // 16)
-                    elif w and w2 and kind == "d" and ops[j][4] == "d" and name in ("qw", "au1", "au2") and rd \
-                            and ops[j][2] and ops[j][2][0][0] == rd[0][0]:
-                        hit = False
                     else:
                         hit = (w or w2) and a < b2 and a2 < b
-                    if hit and need.get(src[j], -1) < j:
+                    if hit:
                         need[src[j]] = j
         for regions, w in ((rd, False), (wr, True)):
-            for name, a, b in regions:
-                seen.setdefault(name, []).append((i, w, a, b))
+            for name, a, b, m in regions:
+                seen.setdefault(name, []).append((i, w, a, b, m))
         if kind == "arr":
             clock[i] = {i: i}
             continue

from concourse.bass import DstId, RemoteDMATransfer
from concourse.mybir import AluOpType, ActivationFunctionType

V, W, G, R, CAP, J, JP, JW = 3136, 4096, 320, 1024, 256, 196, 208, 224
TE = 32
UNIT = 4096.0
MAGIC = 201326592.0
SH = 16384
BF, F32, I32, U16, F16 = "bfloat16", "float32", "int32", "uint16", "float16"
SB = {
    "x1": (W, BF), "x2": (W, BF), "au1": (W, BF), "au2": (W, BF), "bu": (W, BF), "al": (W, BF), "bl": (W, BF),
    "qw": (W, BF), "qn": (2 * W + CAP, BF), "pcj": (J, I32), "pc16": (J, U16), "sf": (512, F32), "q2u": (W, BF), "q2l": (W, BF), "q4": (V, BF), "ww": (V + 16, BF), "abu": (V, BF), "abl": (V, BF),
    "cu": (V, BF), "cl": (V, BF), "pt": (2 * V + CAP, F32),
    "rli": (R, I32), "rlf": (R + CAP, F32), "yc": (W, BF), "mx": (2048, BF), "abd": (2048, BF),
    "si": (512, I32), "ya": (512, F32), "digb": (1024, BF), "idq": (128, BF), "idqn": (128, BF), "crb": (256, BF),
    "q16": (512, U16), "pi16": (512, U16), "eb": (512, BF),
    "p2u": (J, U16), "p2l": (J, U16), "p4u": (J, U16), "p4l": (J, U16),
    "one": (144, BF), "idb": (128, BF), "idn": (128, BF), "id256": (128, BF), "id16": (128, BF),
    "m0": (128, BF), "lm": (128, BF), "m16": (128, BF), "mr": (128, BF), "lb1": (128, BF),
    "idk": (128, F32), "idkn": (128, F32), "la": (128, F32), "thru": (J, F32), "dus": (J, F32),
    "zz": (144, BF), "zu1": (144, BF), "zu3": (144, BF), "zr": (144, BF), "big": (1, BF),
    "g16": (8, BF), "g32": (8, BF), "gn16": (8, BF), "kpat": (256, BF), "zero": (128, BF), "n64": (256, BF),
    "pci": (8, I32), "col": (16, F32), "dd": (256, F32), "nm": (256, BF), "rsbig": (256, F32), "trow": (256, BF),
    "trm": (256, BF), "dump": (64, F32), "li": (16, I32), "l16": (16, U16), "gi": (64, I32),
    "thi": (8, I32), "sni": (60, I32), "sn16": (60, U16), "sbuf": (3 * G, BF),
    "bad": (JP, BF), "sc": (JW, BF), "ul": (JW, BF), "key": (JW, F32), "hh": (JW, F32), "ra": (J, F32),
    "bw": (JW, F32), "cm1": (256, BF), "cm2": (256, BF), "ee": (256, BF), "zh": (256, F16),
    "a16": (16, U16), "j16": (16, U16), "h16": (16, U16), "v16": (16, U16), "of16": (32, U16),
    "tiny": (96, F32), "val": (16, BF), "tj": (256, BF), "te": (256, BF), "xh": (256, F32), "eq": (512, BF),
    "ca16": (256, U16), "caf": (256, F32), "cah": (256, F16), "wv": (256, BF), "dv": (256, F32),
    "pm": (256, F32), "pmx": (256, F32), "oh": (256, BF), "zc": (256, F32), "zch": (256, F16), "zd": (256, F32),
    "crow": (256, F32), "cnt": (8, F32),
}
SCRATCH = {k: ("sbuf", [128, n], d) for k, (n, d) in SB.items()}
PSUM = {"ps0": ("psa", 0), "ps1": ("psa", 512), "ps2": ("psb", 0), "ps3": ("psb", 512)}
SCRATCH["psa"] = ("psum", [128, 1024], F32)
SCRATCH["psb"] = ("psum", [128, 1024], F32)
for _b in range(4, 8):
    SCRATCH["ps%d" % _b] = ("psum", [128, 512], F32)
    PSUM["ps%d" % _b] = ("ps%d" % _b, 0)
NDMA = 120
SEMAPHORES = ["sv", "sa", "st", "sg", "arr", "sent"] + ["d%d" % _i for _i in range(NDMA)]
SIZE = {BF: 2, F32: 4, I32: 4, U16: 2, F16: 2}
ALL = (1 << 128) - 1
A = AluOpType
AF = ActivationFunctionType
XCH = [(0, 48), (48, 72), (72, 98), (98, 146), (146, J)]
HALF = [(0, 98), (98, J)]
FIRST = [(0, 64), (64, J)]
NAT = [(0, 56), (56, 96), (96, 148), (148, J)]
THIRD = [(0, 64), (64, 128), (128, J)]
LCH = [(a, a + 32) for a in range(0, 160, 32)] + [(160, 180), (180, J)]
LSUM = [(2, 0, 64), (6, 64, 128), (6, 128, J)]
LMERGE = [(3, 0, 128), (6, 128, J)]


def rank_program(g, core, T, topo):
    rank = T.rank_of(core)
    if rank is None:
        return
    N = len(T.cores)
    ops = []

    def S(name, a=None, b=None, st=None, p=None):
        nm, o = PSUM.get(name, (name, 0))
        n, sz = (512, 4) if name in PSUM else (SB[name][0], SIZE[SB[name][1]])
        a = 0 if a is None else a
        b = n if b is None else b
        ps = slice(None) if p is None else p
        mask = ALL if p is None else sum(1 << i for i in range(128)[p])
        ap = T[nm][ps, o + a:o + b] if st is None else T[nm][ps, o + a:o + b:st]
        return (ap, [(name, a * sz, b * sz, mask)])

    def P2(i, n):
        return (T["psa" if i == 0 else "psb"][:, 0:n], [("ps%d" % (2 * i + k), 0, 2048, ALL) for k in range(-(-n // 512))])

    def REV(name):
        return (T[name][:, ::-1], S(name)[1])

    def ROW(name, r, a, b):
        return S(name, a, b, p=slice(r, 128, 16))

    def IX(win, off):
        return (win[0].indirect(off[0]), win[1] + off[1], win[1], off[1])

    def H(ap):
        return (ap, [])

    def val(x):
        return x[0] if isinstance(x, tuple) else x

    def add(q, fn, outs, ins, kind="c"):
        rd, wr = [], []
        for x in ins:
            if isinstance(x, tuple):
                rd += x[1]
        for o in outs:
            if len(o) == 4:
                wr += o[2]
                rd += o[3]
            else:
                wr += o[1]
        ops.append((q, fn, rd, wr, kind))

    def vcopy(o, i):
        add("v", lambda: g.vector.tensor_copy(o[0], i[0]), [o], [i])

    def vtt(o, a, b, op):
        add("v", lambda: g.vector.tensor_tensor(o[0], a[0], b[0], op), [o], [a, b])

    def vts(o, a, s1, op0, s2=None, op1=None):
        if op1 is None:
            add("v", lambda: g.vector.tensor_scalar(o[0], a[0], val(s1), None, op0), [o], [a, s1])
        else:
            add("v", lambda: g.vector.tensor_scalar(o[0], a[0], val(s1), val(s2), op0, op1), [o], [a, s1, s2])

    def vscan(o, d0, d1, op0, op1):
        add("v", lambda: g.vector.tensor_tensor_scan(o[0], d0[0], d1[0], 0.0, op0, op1), [o], [d0, d1])

    def act(o, i, f=AF.Identity, bias=0.0, scale=1.0):
        add("a", lambda: g.scalar.activation(o[0], i[0], f, bias=val(bias), scale=val(scale)), [o], [i, bias, scale])

    def mm(o, l, r, start=True, stop=True):
        add("t", lambda: g.tensor.matmul(o[0], l[0], r[0], start, stop), [o], [l, r])

    def iota(o, pat, base, ch=0):
        if SB[o[1][0][0]][1] == I32:
            add("g", lambda: g.iota(o[0], pat, base, ch), [o], [])
        else:
            add("g", lambda: g.iota(o[0], pat, base, ch, allow_small_or_imprecise_dtypes=True), [o], [])

    def fill(o, c):
        iota(o, [[0, o[0].shape[1]]], c)

    def sel(o, i, pat, cmp, fl, base, ch):
        add("g", lambda: g.affine_select(o[0], i[0], pat, cmp, fl, base, ch), [o], [i])

    def rows(o, i, lo, hi):
        n = o[0].shape[1]
        nb, wd = (8, 1) if n == 8 else (n // 16, 16)
        sel(o, i, [[-16, nb], [0, wd]], A.is_ge, 0.0, -lo, 1)
        sel(o, o, [[16, nb], [0, wd]], A.is_ge, 0.0, hi, -1)

    def dma(q, o, i, accumulate=False):
        eng = {"s": g.sync, "a": g.scalar, "g": g}[q]
        if accumulate:
            add(q, lambda: eng.dma_start(o[0], i[0], accum_op=A.add), [o], [i, o], "d")
        else:
            add(q, lambda: eng.dma_start(o[0], i[0]), [o], [i], "d")

    def wrap(o, z, src, a, n, start=True, stop=True):
        for r in range(16):
            mm(o, S(z, 15 - r, 143 - r), S(src, a + r, a + 16 * n, 16), start and r == 0, stop and r == 15)

    add("x", None, [S("x2", V, W)], [], "arr")

    dma("s", S("si", 0, J), H(T.up[:, :]))
    dma("a", S("si", 256, 256 + J), H(T.lo[:, :]))
    dma("s", S("x1"), H(T.x[:, :]))
    dma("s", S("x2", 0, 16 * XCH[0][1]), H(T.x[:, 0:16 * XCH[0][1]]))
    def clear(a, b):
        add("v", lambda: g.vector.memset(T["qw"][:, a:b], 0.0), [S("qw", a, b)], [])

    iota(S("pci", 0, 1), [[0, 1]], 0, 1)
    iota(S("gi", 0, 60), [[16, 60]], V)
    fill(S("one"), 1)
    sel(S("idb"), S("one", 0, 128), [[-1, 128]], A.is_equal, 0.0, 0, 1)
    rows(S("zz"), S("one"), 0, 15)
    clear(0, 1024)
    vts(S("pci", 4, 5), S("pci", 0, 1), 15, A.bitwise_and)
    clear(1024, 2048)
    vcopy(S("col", 0, 1), S("pci", 4, 5))
    clear(2048, 3072)
    act(S("id256"), S("idb"), scale=256.0)
    act(S("id16"), S("idb"), scale=0.0625)
    act(S("idn"), S("idb"), scale=-1.0)
    for t in range(2):
        vts(S("si", 256 * t + J, 256 * t + 256), S("gi", 0, 60), S("col", 0, 1), A.add)
    clear(3072, W)
    vts(S("ya"), S("si"), -7.5, A.add, MAGIC, A.add)
    vts(S("col", 1, 2), S("col", 0, 1), 1.0 / UNIT, A.mult)
    vts(S("ps2"), S("ya"), -MAGIC, A.add)
    act(S("digb", 0, 512), S("ya"), bias=-MAGIC)
    vts(S("col", 2, 3), S("col", 0, 1), 8.0, A.mult)
    vtt(S("digb", 512, 1024), S("si"), S("ps2"), A.subtract)
    dma("a", ROW("qw", 1, 0, W), S("digb", 0, 256))
    dma("s", ROW("qw", 2, 0, W), S("digb", 512, 768))
    mm(S("ps4"), S("id16"), S("digb", 0, 512), True, False)
    mm(S("ps4"), S("id256"), S("digb", 512, 1024), False, True)
    vcopy(S("q16", 0, 452), S("si", 0, 452))
    vcopy(S("pi16", 0, 452), S("ps4", 0, 452))
    vts(S("big"), S("col", 0, 1), 13.0, A.is_ge, float(SH), A.mult)
    vts(S("col", 3, 4), S("col", 0, 1), 256.0, A.mult)
    dma("a", ROW("qw", 3, 0, W), S("digb", 256, 512))
    dma("s", ROW("qw", 4, 0, W), S("digb", 768, 1024))
    for a, b in XCH[1:]:
        dma("s", S("x2", 16 * a, 16 * b), H(T.x[:, 16 * a:16 * b]))
    sel(S("m0"), S("zz", 0, 128), [[0, 128]], A.is_ge, 0.0, 0, 0)
    sel(S("zz"), S("zz"), [[0, 9], [1, 16]], A.is_equal, 0.0, -15, 0)
    iota(S("dd"), [[0, 16], [-8, 16]], 8)
    iota(S("pcj"), [[1, J]], 0)
    vts(S("pc16"), S("pcj"), S("col", 3, 4), A.add)
    rows(S("zu1"), S("zz"), 1, 2)
    iota(S("q2u", V, W), [[16, 60], [0, 16]], V)
    iota(S("q2l", V, W), [[0, 60], [1, 16]], 0)
    rows(S("zu3"), S("zz"), 3, 4)
    for r in (2, 4):
        dma("s", ROW("q2u", r, V, W), ROW("q2l", r, V, W))
    for r in (1, 3):
        dma("s", ROW("q2l", r, V, W), ROW("q2u", r, V, W))
    for nm, src, c in (("zr", "zz", S("col", 0, 1)), ("m16", "m0", 16.0 / UNIT), ("mr", "m0", S("col", 1, 2))):
        act(S(nm), S(src), scale=c)
    for nm, c in (("g16", 16.0), ("g32", 32.0), ("gn16", -16.0)):
        act(S(nm), S("m0", 0, 128, 16), scale=c)
    act(S("nm"), S("dd"), AF.Relu, bias=S("col", 2, 3))
    for nm, ps, c, terms in (("la", "ps0", 1.0, (("idb", 0), ("idb", 2))), ("lb1", "ps1", -16.0, (("idn", 1), ("idb", 2)))):
        for i, (idm, k) in enumerate(terms):
            mm(S(ps, 0, 128), S(idm), S("zz", 15 - k, 143 - k), i == 0, i == 1)
        act(S(nm), S(ps, 0, 128), scale=c)

    def quarters(src, half):
        act(S("eb", 0, 452), S(src, 0, 452), bias=(129.0 - half / 1024) / 4, scale=1.0 / UNIT)

    def classes(rnd, ps, n, ide):
        if rnd == 0:
            terms = [("idq", "digb", 0), ("idq", "digb", 512), ("idq" + n, "digb", 256), ("idq" + n, "digb", 768)]
        else:
            terms = [("idk", "sf", 0), ("idk" + n, "sf", 256)]
        for i, (idm, src, a) in enumerate(terms + [("idn", "eb", 0), (ide, "eb", 256)]):
            mm(S(ps, 0, J), S(idm), S(src, a, a + J), i == 0, False)

    def natural(q, a, b):
        o, i = S("qn", 16 * a, 16 * b), IX(S("qw"), S("pc16", a, b))
        if q == "v":
            vcopy(o, i)
        else:
            act(o, i)

    def lower(a, b):
        for r in (1, 2):
            dma("s", ROW("qn", r, W + a, W + b), ROW("qn", r + 2, a, b))

    quarters("digb", 504.0)

    def constants():
        dma("s", S("thi", 0, 1), H(T.th[:, :]))
        dma("s", S("sni"), H(T.snd[:, :]))
        dma("s", S("au1", V, W), H(T.x[:, V:W]))
        fill(S("zero"), 0)
        for nm, c in (("idq", 1.0 / UNIT), ("idqn", -1.0 / UNIT), ("idk", 1.0 / UNIT), ("idkn", -1.0 / UNIT)):
            sel(S(nm), S("zero"), [[-1, 128]], A.not_equal, c, 0, 1)
        sel(S("lm"), S("m0"), [[1, 128]], A.is_gt, 0.0, 0, -1)
        sel(S("lm"), S("lm"), [[1, 128]], A.not_equal, -256.0, 0, -1)
        iota(S("trow"), [[1, 256]], 0)
        iota(S("trm"), [[1, 256]], -256)
        for nm, a, b, c in (("bad", J, JP, 0), ("sc", 0, 8, 0), ("ul", J, JW, 0), ("key", J, JW, 0), ("hh", J, JW, 0),
                            ("bw", 0, JW, SH), ("ww", V, V + 16, 0), ("rlf", R, R + CAP, 0), ("n64", 0, 256, -65)):
            fill(S(nm, a, b), c)
        iota(S("kpat"), [[0, 16], [1, 16]], 0)
        fill(S("rsbig"), 0)
        sel(S("rsbig"), S("rsbig"), [[0, 16], [1, 16]], A.not_equal, 1048576.0, 0, 0)
        iota(S("li"), [[1, 16]], 0)
        iota(S("dump", 0, 16), [[16, 16]], R - SH)
        iota(S("dump", 16, 32), [[16, 16]], 2 * W - SH)
        iota(S("dump", 32, 48), [[16, 16]], R - SH)
        iota(S("dump", 48, 64), [[16, 16]], 2 * V - SH)
        fill(S("qn", W, 2 * W + CAP), 0)

    def level(o, src, own, lst, base, a, b, copy=None):
        vtt(S(o, 16 * a, 16 * b), IX(S(src), S(lst, base + a, base + b)), S(own, 16 * a, 16 * b), A.max)
        if copy:
            dma("s", S(copy, 16 * a, 16 * b), S(o, 16 * a, 16 * b))

    def chase(o, win, lst, base, z, ps, parts, meanwhile=None):
        for a, b in parts:
            act(S(o, 16 * a, 16 * b), IX(win, S(lst, base + a, base + b)))
            if meanwhile:
                meanwhile()
            wrap(S(ps, a, b), z, o, 16 * a, b - a)

    def minus(i, m, a, b):
        for idm, src in (("idn", "ww"), ("idb", m)):
            for c in range(16 * a, 16 * b, 512):
                e = min(c + 512, 16 * b)
                mm(S("ps%d" % (2 * i + (c - 16 * a) // 512), 0, e - c), S(idm), S(src, c, e), src == "ww", src != "ww")

    def size(i, ab, a, b):
        act(S(ab, 16 * a, 16 * b), P2(i, 16 * (b - a)), AF.Abs)

    def merge(au, a, b):
        for k in range(8):
            rw = slice(16 * k + 8, 16 * k + 16)
            dma("s", S(au, a, b, p=rw), S("al", a, b, p=rw))

    def rhyme_write(batches, between):
        for q in batches:
            vtt(IX(S("rlf"), S("of16", 2 * q, 2 * q + 2)), S("zd", 32 * q, 32 * q + 32), S("caf", 32 * q, 32 * q + 32), A.add)
            if between:
                between.pop(0)()

    far = [d for d in range(1, N) if topo.chip(T.cores[(rank + d) % N]) != topo.chip(core)]
    out = topo.engines(core, T.cores[(rank + far[0]) % N])
    per = len(out) // len(far)
    eng = {d: out[per * i:per * i + per] for i, d in enumerate(far)}
    for d in range(1, N):
        if d not in far:
            eng[d] = [e for e in topo.engines(core, T.cores[(rank + d) % N]) if e not in out]
    total = sum(len(eng[d]) for d in eng)

    def send():
        act(S("sbuf"), IX(S("au1"), S("sn16")))
        trs = []
        for d in range(1, N):
            rid, pid, _ = topo.addr(T.cores[(rank + d) % N])
            trs.append(RemoteDMATransfer(dst_ids=[DstId(rid=rid, pnc=pid)], dma_engine_mask=sum(1 << e for e in eng[d]),
                                         remote_sem=T.sem.arr, src=T["sbuf"][:, (d - 1) * G:d * G],
                                         dst=T["x2"][:, V + (d - 1) * G:V + d * G]))
        add("g", lambda: g.remote_dma_fused(trs, local_sem=T.sem.sent), [], [S("sbuf")], "r")

    for rnd in range(2):
        xs, xo, au = ("x1", "x2", "au1") if rnd == 0 else ("x2", "x1", "au2")
        wu, wl, zl, pl = (S("qw"), S("qw"), "zu3", "pi16") if rnd == 0 else (S("qn", 0, W), S("qn", W, 2 * W), "zu1", "q16")
        thr = S("col", 8 + rnd, 9 + rnd)
        if rnd == 0:
            constants()
            for a, b in XCH[:3]:
                level(au, xs, xo, "q16", 0, a, b)
            dma("s", S("cu", 0, 1568), S(au, 0, 1568))
            for a, b in XCH[3:]:
                level(au, xs, xo, "q16", 0, a, b)
            dma("s", S("cu", 1568, V), S(au, 1568, V))
            dma("s", S("bu", V, W), H(T.x[:, V:W]))
            dma("s", S("ww", 0, 1568), H(T.w[:, 0:1568]))
        else:
            for (a, b, o), (c, e) in zip(((0, 64, 0), (64, J, 1024), (256, 256 + J, W)), ((0, 48), (48, 130), (130, J))):
                wrap(S("ps6", a, b), "zu1", "qn", o, b - a)
                vcopy(S("q16", a, b), S("ps6", a, b))
                level(au, xs, xo, "q16", 0, c, e, "cu")
        chase("q2u", wu, pl, 0, "zu1", "ps4", HALF if rnd == 0 else FIRST)
        chase("q2l", wl, pl, 256, zl, "ps5", [(0, 50)])
        level("al", xs, xo, "q16", 256, 0, 50)
        vcopy(S("p2u"), S("ps4", 0, J))
        chase("q4", S("q2u"), "p2u", 0, "zu1", "ps7", HALF)
        level("al", xs, xo, "q16", 256, 50, 122)
        level("al", xs, xo, "q16", 256, 122, J)
        dma("s", S("cl", 0, 2048), S("al", 0, 2048))
        chase("q2l", wl, pl, 256, zl, "ps5", [(50, 122), (122, J)])
        for a, b in THIRD:
            if b == J:
                vcopy(S("p4u"), S("ps7", 0, J))
            level("bu", au, "cu", "p2u", 0, a, b, "cu")
        if rnd == 0:
            dma("s", S("al", V, W), H(T.x[:, V:W]))
            dma("s", S("ww", 1568, V), H(T.w[:, 1568:V]))
        dma("s", S("cl", 2048, V), S("al", 2048, V))
        if rnd == 0:
            dma("s", S("bl", V, W), H(T.x[:, V:W]))
            natural("a", *NAT[0])
        else:
            act(S("sf", 0, 452), S("ps6", 0, 452))
            quarters("sf", 511.5)
            for t in range(2):
                dma("s", ROW("pt", 0, V * t, V * t + V), S("sf", 256 * t, 256 * t + J))
        level(au, "bu", "cu", "p4u", 0, 0, 32)
        vcopy(S("p2l"), S("ps5", 0, J))
        level(au, "bu", "cu", "p4u", 0, 32, 98)
        level(au, "bu", "cu", "p4u", 0, 98, J)
        classes(rnd, "ps4", "n", "idb")
        classes(rnd, "ps7", "", "idn")
        def first():
            minus(0, au, 0, 49)
            minus(1, au, 49, 98)

        def second():
            minus(0, au, 98, 147)
            minus(1, au, 147, J)
            wrap(S("ps5", 0, 98), "zz", "abu", 0, 98)

        chase("q4", S("q2l"), "p2l", 0, zl, "ps6", HALF[:1], first)
        size(0, "abu", 0, 49)
        size(1, "abu", 49, 98)
        chase("q4", S("q2l"), "p2l", 0, zl, "ps6", HALF[1:], second)
        size(0, "abu", 98, 147)
        size(1, "abu", 147, J)
        if rnd == 0:
            dma("s", S("rli"), H(T.rl[:, :]))
        for a, b in THIRD:
            level("bl", "al", "cl", "p2l", 0, a, b, "cl")
        vcopy(S("p4l"), S("ps6", 0, J))
        if rnd == 0:
            sel(S("rlf", 0, R), S("rli"), [[0, R]], A.is_ge, 0.0, 0, 0)

        def piece(i):
            return S("ps%d" % (i % 4), 0, 16 * (LCH[i][1] - LCH[i][0]))

        def witness(i):
            if i < len(LCH):
                mm(piece(i), S("idn"), S("ww", 16 * LCH[i][0], 16 * LCH[i][1]), True, False)

        for i in range(3):
            witness(i)
        wrap(S("ps5", 98, J), "zz", "abu", 1568, 98)
        for i, (a, b) in enumerate(LCH):
            level("al", "bl", "cl", "p4l", 0, a, b)
            mm(piece(i), S("idb"), S("al", 16 * a, 16 * b), False, True)
            act(S("abl", 16 * a, 16 * b), piece(i), AF.Abs)
            witness(i + 3)
            for after, c, e in LSUM:
                if after == i:
                    wrap(S("ps6", c, e), "zz", "abl", 16 * c, e - c)
            for after, c, e in LMERGE:
                if after == i:
                    merge(au, 16 * c, 16 * e)
        def upper_sums():
            return [lambda: vts(S("thru"), S("ps5", 0, J), -1.0, A.mult, thr, A.add), lambda: vcopy(S("dus"), S("ps5", 0, J))]

        if rnd == 0:
            vcopy(thr, S("thi", 0, 1))
            vcopy(S("sn16"), S("sni"))
            for f in upper_sums():
                f()
            natural("v", *NAT[1])
            natural("a", *NAT[2])
        else:
            rhyme_write(range(6, 3, -1), upper_sums())
        vtt(S("bad", 0, J), S("ps6", 0, J), S("thru"), A.is_gt)
        vscan(S("sc", 8, 8 + JP), S("bad"), S("bad"), A.add, A.max)
        vtt(S("ul", 0, J), S("ps6", 0, J), S("dus"), A.is_le)
        if rnd == 1:
            dma("s", H(T.y[:, :]), S(au, 0, V))
        else:
            send()
            dma("s", S("qn", V, W), S("q2u", V, W))
            lower(0, 16 * NAT[2][1])
            lower(V, W)
        mm(S("ps0", 0, 1), S("idb"), S("big"), True, False)
        for a in range(13):
            mm(S("ps0", 0, 1), S("zz", 15 - a, 143 - a), S("sc", 16 * a + 23, 16 * a + 24), False, a == 12)
        wrap(S("ps1", 0, 13), "zz", "sc", 8, 13)
        vts(S("cm1"), S("trow"), S("ps0", 0, 1), A.is_ge, 16.0, A.mult)
        if rnd == 1:
            rhyme_write([3, 2], [])
        else:
            vts(S("dump"), S("dump"), S("col", 0, 1), A.add, 1.0 / SH, A.mult)
            vcopy(S("l16"), S("li"))
        act(S("bw", 0, JP, 16), S("ps1", 0, 13))
        wrap(S("ps3", 0, 16), "zz", "cm1", 0, 16)
        mm(S("ps2", 0, J), S("m0"), S("sc", 7, 7 + J), True, False)
        mm(S("ps2", 0, J), S("lm"), S("bad", 0, J), False, True)
        mm(S("ps4", 0, J), S("idb"), S("ul", 0, J), False, True)
        wrap(S("ps5", 0, 16), "zz", "cm1", 0, 16, True, False)
        vcopy(S("a16"), S("ps3", 0, 16))
        vtt(S("cm2"), IX(S("bw"), S("a16")), S("trow"), A.is_le)
        if rnd == 1:
            rhyme_write([1, 0], [])
        act(S("key", 0, J), S("ps2", 0, J))
        act(S("ra"), S("ps4", 0, J), AF.Abs, bias=-UNIT / 2, scale=UNIT)
        wrap(S("ps5", 0, 16), "zz", "cm2", 0, 16, False, True)
        mm(S("ps7", 0, J), S("idk"), S("ra"), False, True)
        vcopy(S("j16"), S("ps5", 0, 16))
        act(S("tiny", 0, 16), S("ps5", 0, 16), scale=16.0 * UNIT)
        act(S("hh", 0, J), S("ps7", 0, J), bias=258.0 * 512 - 1023.0, scale=UNIT / 2)
        if rnd == 1:
            act(S("tiny", 16, 32), S("ps5", 0, 16), scale=-3135.0 * UNIT / SH)
        vtt(S("ee"), IX(S("key"), S("j16")), S("trm"), A.is_equal)
        vtt(S("zh"), IX(S("hh"), S("j16")), S("ee"), A.mult)
        act(S("tj"), IX(S("ul"), S("j16")))
        mm(S("ps1", 0, 16), S("idk"), S("tiny", 0, 16), True, False)
        wrap(S("ps1", 0, 16), "zr", "ee", 0, 16, False, True)
        wrap(S("ps0", 0, 16), "zz", "zh", 0, 16)
        vts(S("v16"), S("ps1", 0, 16), float(V), A.min)
        act(S("wv"), IX(S("ww"), S("v16")))
        act(S("tiny", 32, 48), S("ps1", 0, 16), scale=(1.0, 196.0)[rnd] * UNIT / SH)
        vts(S("h16"), S("ps0", 0, 16), -1.0, A.add)
        vcopy(S("ca16"), IX(S("rlf"), S("h16")))
        act(S("tiny", 48, 64), S("ps0", 0, 16), bias=-UNIT / SH, scale=UNIT / SH)
        act(S("val"), S("ps0", 0, 16), AF.Sign)
        act(S("xh"), IX(S("tiny", 48, 64), S("l16")), bias=1.0, scale=SH / UNIT)
        act(S("caf"), IX(S("rlf"), S("h16")))
        mm(S("ps7", 0, 256), S("id256"), S("nm"), True, False)
        mm(S("ps7", 0, 256), S("m0"), S("zh"), False, True)
        mm(S("ps7", 256, 496), S("m0"), S("zh", 16, 256))
        mm(S("ps6", 0, 128), S("idb"), S("wv", 0, 128))
        mm(S("ps4", 0, 256), S("idb"), S("kpat"), True, False)
        mm(S("ps5", 0, 256), S("idb"), S("ee"), True, False)
        mm(S("ps5", 0, 256), S("idn"), S("tj"), False, True)
        mm(S("ps6", 256, 512), S("m16"), S("cm1"), True, False)
        mm(S("ps6", 256, 512), S("m16"), S("cm2"), False, False)
        mm(S("ps6", 256, 512), S("mr"), S("ee"), False, False)
        mm(S("ps6", 256, 512), S("idkn"), S("caf"), False, True)
        vcopy(S("yc", 0, 16 * TE), IX(S(au), S("ca16", 0, TE)))
        vtt(S("eq", 0, 256), S("ps7", 0, 256), S("xh"), A.is_equal)
        vtt(S("eq", 256, 496), S("ps7", 256, 496), S("xh", 0, 240), A.is_equal)

        def places(ps, a):
            vtt(S("tiny", 64 + a, 80 + a), S(ps, 0, 16), S("dump", 32 * rnd + a, 32 * rnd + a + 16), A.min)
            return lambda: vts(S("of16", a, a + 16), S("tiny", 64 + a, 80 + a), 1.0, A.add, float(SH), A.mult)

        def differ(c, witness):
            for k in range(16):
                ps = "ps%d" % (2 * c + k // 8)
                o = S(ps, 64 * (k % 8), 64 * (k % 8) + 64)
                if witness and k % 8 == 0:
                    mm(S(ps), S("zero"), S("ww", 0, 512), True, False)
                if witness:
                    mm(o, S("idn"), S("wv", 128 + 64 * c, 192 + 64 * c), False, False)
                else:
                    mm(o, S("idb"), S("yc", 2048 + 1024 * c + k, 3072 + 1024 * c, 16), False, k % 8 == 7)

        def keys(c, ks, stop=False):
            for k in ks:
                if c < 2:
                    mm(S("ps4", 128 + k, 256, 16, p=slice(64 * c, 64 * c + 64)),
                       S("abd", 1024 * c + 64 * k, 1024 * c + 64 * k + 64), S("g16"), False, stop and k == ks[-1])
                else:
                    mm(S("ps4", k, 128, 16), S("mx", 128 * k, 128 * k + 128), S("g32"), False, stop and k == ks[-1])

        vcopy(S("yc", 16 * TE, 2048), IX(S(au), S("ca16", TE, 128)))
        act(S("yc", 2048, 3072), IX(S(au), S("ca16", 128, 192)))
        act(S("yc", 3072, W), IX(S(au), S("ca16", 192, 256)))
        differ(0, True)
        differ(1, True)
        differ(0, False)
        for k in range(16):
            mm(S("ps4", k, 128, 16), S("yc", k, 2048, 16), S("gn16"), False, False)
        differ(1, False)
        act(S("abd", 0, 1024), P2(0, 1024), AF.Abs)
        act(S("abd", 1024, 1536), S("ps2"), AF.Abs)
        act(S("abd", 1536, 2048), S("ps3"), AF.Abs)
        act(S("te"), S("ps5", 0, 256), AF.Relu, scale=float((W, V)[rnd]) / SH)
        for k in range(16):
            vtt(S("mx", 128 * k, 128 * k + 128), S("ps6", 0, 128), S("yc", k, 2048, 16), A.max)
        keys(0, range(16))
        keys(2, range(8))
        keys(1, range(8))
        keys(2, range(8, 15))
        keys(1, range(8, 16))
        keys(2, [15], True)
        act(S("dv"), S("ps6", 256, 512), scale=UNIT)

        def rhyme_places():
            mm(S("ps7", 0, 16), S("idk"), S("tiny", 48, 64), True, False)
            mm(S("ps7", 0, 16), S("idn"), S("val"), False, False)
            wrap(S("ps7", 0, 16), "zz", "eq", 0, 16, False, False)
            wrap(S("ps7", 1, 16), "zz", "eq", 256, 15, False, True)

        def table_places():
            mm(S("ps5", 0, 16), S("idn"), S("val"), True, False)
            wrap(S("ps5", 0, 16), "zz", "te", 0, 16, False, False)
            if rnd == 1:
                mm(S("ps5", 0, 16), S("idk"), S("tiny", 16, 32), False, False)
            mm(S("ps5", 0, 16), S("idk"), S("tiny", 32, 48), False, True)

        if rnd == 0:
            natural("a", *NAT[3])
            lower(16 * NAT[3][0], V)
            vts(S("cah"), S("caf"), 0.0625, A.mult, 1039.53125, A.add)
            mm(S("ps0", 0, 256), S("lb1"), S("n64"), True, False)
            table_places()
        else:
            rhyme_places()
        vscan(S("ps1", 0, 256), S("rsbig"), S("ps4", 0, 256), A.add, A.min)
        vscan(REV("pmx"), S("rsbig"), (T["ps4"][:, 255::-1], S("ps4", 0, 256)[1]), A.add, A.min)
        vtt(S("oh"), S("ps1", 0, 256), S("pmx"), A.is_equal)
        for h in range(2):
            mm(S("ps6", 128 * h, 128 * h + 128), S("oh", 128 * h, 128 * h + 128), S("idb"))
        then = places("ps5", 16) if rnd == 0 else places("ps7", 0)
        then()
        if rnd == 0:
            vtt(S("zc"), S("ps6", 0, 256), S("caf"), A.mult)
            vtt(S("zch"), S("ps6", 0, 256), S("cah"), A.mult)
            mm(S("ps0", 0, 256), S("la"), S("zc"), False, False)
            mm(S("ps0", 0, 256), S("lb1"), S("zch"), False, True)
            rhyme_places()
            vtt(S("zd"), S("ps6", 0, 256), S("dv"), A.mult)
            act(S("crb"), S("ps0", 0, 256))
            vcopy(IX(S("qn"), S("of16", 16, 32)), S("crb"))
            places("ps7", 0)()
            rhyme_write([7], [])
            for b in ("au2", "al", "bu", "bl"):
                dma("s", S(b, V, W), S("x2", V, W))
            mm(S("ps1", 0, 1), S("one", 0, 128), S("sc", 7 + JP, 8 + JP))
            act(S("cnt", 1, 2), S("ps1", 0, 1), bias=-7.5)
            act(S("cnt", 2, 3), S("cnt", 1, 2), bias=MAGIC)
            act(S("cnt", 3, 4), S("cnt", 2, 3), bias=MAGIC, scale=-1.0)
            act(S("cnt", 4, 5), S("ps1", 0, 1), bias=S("cnt", 3, 4))
            act(S("col", 9, 10), S("cnt", 4, 5), bias=S("col", 8, 9))
        else:
            def chosen():
                vtt(S("zc"), S("ps6", 0, 256), S("caf"), A.mult)
                mm(S("ps0", 0, 256), S("la"), S("zc"))
                act(S("crow"), S("ps0", 0, 256))

            def table(a, b):
                return lambda: vcopy(IX(S("pt"), S("of16", 16 + a, 16 + b)), S("crow", 16 * a, 16 * b))

            def pointers():
                table(12, 16)()
                dma("s", H(T.up1[:, :]), ROW("pt", 0, 0, V))
                dma("a", H(T.lo1[:, :]), ROW("pt", 0, V, 2 * V))

            table_places()
            chosen()
            vtt(S("zd"), S("ps6", 0, 256), S("dv"), A.mult)
            later = [places("ps5", 16)]
            rhyme_write(range(7, -1, -1), later + [lambda: None, table(0, 4), table(4, 8), table(8, 12), pointers])
            dma("s", H(T.rl1[:, 0:512]), S("rlf", 0, 512))
            dma("a", H(T.rl1[:, 512:R]), S("rlf", 512, R))

    emit(g, T, ops, total)


def emit(g, T, ops, total):
    queue = {"v": g.vector, "a": g.scalar, "t": g.tensor, "g": g, "s": g.sync}
    csem = {"v": T.sem.sv, "a": T.sem.sa, "t": T.sem.st, "g": T.sem.sg}
    src = [o[0] if o[4] == "c" else i for i, o in enumerate(ops)]
    seen, known, clock, waits = {}, {q: {} for q in queue}, [None] * len(ops), [[] for _ in ops]
    for i, (q, fn, rd, wr, kind) in enumerate(ops):
        need = {}
        for regions, w in ((rd, False), (wr, True)):
            for name, a, b, m in regions:
                psum = name in PSUM
                for j, w2, a2, b2, m2 in seen.get(name, []):
                    if need.get(src[j], -1) >= j:
                        continue
                    same = ops[j][4] == "c" and kind == "c" and ops[j][0] == q
                    if psum and not same:
                        hit = True
                    elif (same and q == "t") or not m & m2:
                        hit = False
                    elif w and w2 and (kind == "c") != (ops[j][4] == "c"):
                        hit = a // 16 < -(-b2 // 16) and a2 // 16 < -(-b // 16)
                    else:
                        hit = (w or w2) and a < b2 and a2 < b
                    if hit:
                        need[src[j]] = j
        for regions, w in ((rd, False), (wr, True)):
            for name, a, b, m in regions:
                seen.setdefault(name, []).append((i, w, a, b, m))
        if kind == "arr":
            clock[i] = {i: i}
            continue
        kn = known[q]
        for j in sorted(need.values(), reverse=True):
            if kn.get(src[j], -1) >= j:
                continue
            waits[i].append(j)
            for s, k in clock[j].items():
                if kn.get(s, -1) < k:
                    kn[s] = k
        clock[i] = dict(kn)
        clock[i][src[i]] = i
    last = {}
    for i, o in enumerate(ops):
        if o[4] == "c":
            last[o[0]] = i
    used = set(j for ws in waits for j in ws) | set(last.values())
    token, count, nd = {}, {q: 0 for q in csem}, 0
    for i, (q, fn, rd, wr, kind) in enumerate(ops):
        if kind == "arr":
            token[i] = (T.sem.arr, total)
            continue
        for j in waits[i]:
            queue[q].wait_ge(token[j][0], token[j][1])
        ins = fn()
        if kind == "d":
            token[i] = (T.sem["d%d" % nd], 16)
            nd += 1
            ins.then_inc(token[i][0], 16)
        elif kind == "r":
            token[i] = (T.sem.sent, total)
        elif i in used:
            count[q] += 1
            token[i] = (csem[q], count[q])
            ins.then_inc(csem[q], 1)
    done = set(j for ws in waits for j in ws)
    for i, o in enumerate(ops):
        if (o[4] != "c" and i not in done) or (o[4] == "c" and last[o[0]] == i):
            g.sync.wait_ge(token[i][0], token[i][1])
